import numpy as np
import ml_dtypes


def mxq(x, axis, fmt="e4m3"):
    dtype, down = {"e4m3": (ml_dtypes.float8_e4m3fn, 7), "e5m2": (ml_dtypes.float8_e5m2, 14)}[fmt]
    v = np.moveaxis(np.asarray(x, np.float32).astype(ml_dtypes.bfloat16).astype(np.float64), axis, -1)
    blocks = v.reshape(v.shape[:-1] + (-1, 32))
    amax = np.abs(blocks).max(-1, keepdims=True)
    byte = np.maximum(np.where(amax > 0, np.frexp(amax)[1] - 1 + 127, 0) - down, 1)
    scale = np.exp2(byte - 127.0)
    codes = (blocks / scale).astype(np.float32).astype(dtype).astype(np.float64)
    return np.moveaxis((codes * scale).reshape(v.shape), -1, axis)


WIDE = False


def mx_kscale(k):
    if not WIDE:
        return np.ones(k)
    levels = np.array([18, -18])
    if k % 512:
        return np.exp2(np.random.permutation(np.resize(levels, k // 32))).repeat(32)
    a = np.empty((k // 512, 16))
    for p in range(k // 512):
        a[p, :8] = np.random.permutation(np.resize(levels, 8))
        for g in range(8):
            far = levels[np.abs(levels - a[p, g]) >= 10]
            a[p, g + 8] = far[np.random.randint(len(far))]
    return np.exp2(a.ravel()).repeat(32)


def f64(x):
    return np.asarray(x).astype(np.float64)


def striped(idx):
    return np.tile(np.asarray(idx).reshape(-1, 16).T, (8, 1)).astype(np.uint16)


def unstriped(offs):
    return offs[:16].T.reshape(-1).astype(np.int64)


def setup_inputs():
    n = np.random.standard_normal
    uni = np.random.uniform
    src = np.random.randint(0, 512, 1024)
    dst = np.random.randint(0, 512, 1024)
    f_d = mx_kscale(512)
    return {
        "W": (n((512, 512)) / np.sqrt(512) * f_d[:, None]).astype(np.float32),
        "hT": (n((512, 512)) / f_d[:, None]).astype(np.float32),
        "dyT": (n((512, 512)) / np.sqrt(512)).astype(np.float32),
        "soffs": striped(src),
        "toffs": striped(dst),
    }


def reference(W, hT, dyT, soffs, toffs):
    src = unstriped(soffs)
    dst = unstriped(toffs)
    u = mxq(f64(W), 0, "e4m3").T @ mxq(f64(hT), 0, "e4m3")
    us = u[:, src]
    ds = f64(dyT)[:, dst]
    q = us * ds
    qt = q.T
    s = (qt).sum(-1, keepdims=True)
    out = s.T
    return out

@@ -1,0 +1,145 @@
+from contextlib import ExitStack
+
+import concourse.mybir as mybir
+from concourse.masks import make_identity
+
+F32 = mybir.dt.float32
+BF16 = mybir.dt.bfloat16
+U32 = mybir.dt.uint32
+U16 = mybir.dt.uint16
+U8 = mybir.dt.uint8
+FP8X4 = mybir.dt.float8_e4m3fn_x4
+
+P = 128
+PACK = 4
+D, M, X, C = 512, 512, 512, 1024
+HALF = 256
+PAD = 8
+EDGES = 512
+BLOCKS = M // P
+FLOPS = 2 * D * M * X + 2 * M * C
+
+
+def tile_attend_gedgew_kernel(tc, W, hT, dyT, soffs, toffs, out):
+    nc = tc.nc
+    mult = mybir.AluOpType.mult
+    add = mybir.AluOpType.add
+    copy = mybir.ActivationFunctionType.Copy
+    with ExitStack() as ctx:
+        held = ctx.enter_context(tc.tile_pool(name="held", bufs=1))
+        psum = ctx.enter_context(tc.psum_pool(name="psum", bufs=1))
+
+        toffs_t = held.tile([P, C // 16], U16, name="toffs_t")
+        soffs_t = held.tile([P, C // 16], U16, name="soffs_t")
+        dy = [held.tile([P, X + PAD], F32, name="dy%d" % b) for b in range(BLOCKS)]
+        u = [held.tile([P, X + PAD], F32, name="u%d" % b) for b in range(BLOCKS)]
+        h_raw = [held.tile([P, PACK, HALF], F32, name="h_raw%d" % i, tag="h_raw%d" % i, align_bytes=64) for i in range(2)]
+        w_raw = [held.tile([P, PACK, HALF], F32, name="w_raw%d" % i, tag="w_raw%d" % i, align_bytes=64) for i in range(2)]
+        h_rows = hT.rearrange("(p j) x -> p j x", j=PACK)
+        w_rows = W.rearrange("(p j) m -> p j m", j=PACK)
+
+        nc.sync.dma_start(dy[0][:, 0:X], dyT[0:P, :])
+        nc.sync.dma_start(toffs_t[:], toffs)
+        nc.sync.dma_start(h_raw[0][:], h_rows[:, :, 0:HALF])
+        nc.sync.dma_start(dy[1][:, 0:X], dyT[P : 2 * P, :])
+        nc.sync.dma_start(h_raw[1][:], h_rows[:, :, HALF : 2 * HALF])
+        nc.sync.dma_start(dy[2][:, 0:X], dyT[2 * P : 3 * P, :])
+        nc.sync.dma_start(w_raw[0][:], w_rows[:, :, 0:HALF])
+        nc.sync.dma_start(w_raw[1][:], w_rows[:, :, HALF : 2 * HALF])
+        nc.sync.dma_start(dy[3][:, 0:X], dyT[3 * P : 4 * P, :])
+        nc.sync.dma_start(soffs_t[:], soffs)
+
+        for b in range(BLOCKS):
+            nc.vector.memset(dy[b][:, X : X + PAD], 0.0)
+        for b in range(BLOCKS):
+            nc.vector.memset(u[b][:, X : X + PAD], 0.0)
+        ident = held.tile([P, P], F32, name="ident")
+        make_identity(nc, ident[:])
+        sums = held.tile([P, P], F32, name="sums")
+        nc.gpsimd.memset(sums[:], 0.0)
+
+        h_codes = held.tile([P, X], U32, name="h_codes", align_bytes=64)
+        h_scales = held.tile([P, X], U8, name="h_scales", align_bytes=64)
+        w_codes = held.tile([P, M], U32, name="w_codes", align_bytes=64)
+        w_scales = held.tile([P, M], U8, name="w_scales", align_bytes=64)
+
+        def quantise(raw, tag, codes, scales):
+            grouped = held.tile([P, HALF, PACK], BF16, name=tag, tag=tag, align_bytes=64)
+            nc.scalar.copy(
+                out=grouped[:].rearrange("p (c i) t -> p c t i", i=4),
+                in_=raw[:].rearrange("p t (c i) -> p c t i", i=4),
+            )
+            nc.vector.quantize_mx(
+                out=codes.bitcast(FP8X4), scales=scales, in_=grouped[:].rearrange("p w j -> p (w j)")
+            )
+
+        def gather_dy(b, e, tag):
+            g = held.tile([P, EDGES], F32, name="dg%d_%d" % (b, e), tag=tag, align_bytes=64)
+            cols = slice(e * EDGES // 16, (e + 1) * EDGES // 16)
+            nc.vector.tensor_copy(g[:], dy[b][:].indirect(toffs_t[:, cols]))
+            return g
+
+        dg = {}
+        for b in range(2):
+            for e in range(2):
+                dg[b, e] = gather_dy(b, e, "dg%d_%d" % (b, e))
+        for i in range(2):
+            cols = slice(i * HALF, (i + 1) * HALF)
+            quantise(h_raw[i], "hb%d" % i, h_codes[:, cols], h_scales[:, cols])
+            dg[2, i] = gather_dy(2, i, "h_raw%d" % i)
+        for i in range(2):
+            cols = slice(i * HALF, (i + 1) * HALF)
+            quantise(w_raw[i], "wb%d" % i, w_codes[:, cols], w_scales[:, cols])
+            for b in (2 * i, 2 * i + 1):
+                acc = psum.tile([P, X], F32, name="acc%d" % b, tag="bank%d" % b)
+                mc = slice(b * P, (b + 1) * P)
+                nc.tensor.matmul_mx(
+                    out=acc[:],
+                    lhsT=w_codes[:, mc].bitcast(FP8X4),
+                    lhsT_scale=w_scales[:, mc],
+                    rhs=h_codes[:].bitcast(FP8X4),
+                    rhs_scale=h_scales[:],
+                    start=True,
+                    stop=True,
+                )
+                nc.scalar.copy(out=u[b][:, 0:X], in_=acc[:])
+            dg[3, i] = gather_dy(3, i, "w_raw%d" % i)
+
+        junk = held.tile([P, P], F32, name="junk")
+        groups = EDGES // P
+        for e in range(2):
+            turned = [
+                psum.tile([P, P], F32, name="t%d_%d" % (e, g), tag="bank%d" % ((4 + 4 * e + g) % 8))
+                for g in range(groups)
+            ]
+            for b in range(BLOCKS):
+                last = e == 1 and b == BLOCKS - 1
+                pieces = [(0, 256), (256, 128), (384, 128)] if last else [(0, EDGES)]
+                for lo, n in pieces:
+                    q = held.tile([P, n], F32, name="q%d_%d_%d" % (e, b, lo))
+                    c0 = (e * EDGES + lo) // 16
+                    nc.vector.tensor_tensor(
+                        q[:], u[b][:].indirect(soffs_t[:, c0 : c0 + n // 16]), dg[b, e][:, lo : lo + n], mult
+                    )
+                    for k in range(n // P):
+                        g = lo // P + k
+                        nc.tensor.matmul(
+                            turned[g][:],
+                            q[:, k * P : (k + 1) * P],
+                            ident[:],
+                            start=(b == 0),
+                            stop=(b == BLOCKS - 1),
+                            is_transpose=True,
+                        )
+                        if b == BLOCKS - 1:
+                            col = sums[:, e * groups + g : e * groups + g + 1]
+                            if e == 1 and g == groups - 1:
+                                nc.vector.tensor_reduce(col, turned[g][:], mybir.AxisListType.X, add)
+                            else:
+                                nc.scalar.activation(junk[:], turned[g][:], copy, accum_out=col)
+
+        rows = psum.tile([P, P], F32, name="rows", tag="bank4")
+        nc.tensor.transpose(rows[:], sums[:], ident[:])
+        res = held.tile([C // P, P], F32, name="res")
+        nc.vector.tensor_copy(res[:], rows[0 : C // P, :])
+        nc.sync.dma_start(out.rearrange("o (g p) -> (o g) p", p=P), res[:])

@@ -14,9 +14,11 @@ P = 128
 PACK = 4
 D, M, X, C = 512, 512, 512, 1024
 HALF = 256
-PAD = 8
-EDGES = 512
 BLOCKS = M // P
+GROUPS = C // P
+DY_WINDOW = 1376
+U_WINDOW = C + 8
+STEPS = [(0, 0, 1024), (1, 0, 1024), (2, 0, 512), (3, 0, 512), (2, 512, 512), (3, 512, 256), (3, 768, 128), (3, 896, 128)]
 FLOPS = 2 * D * M * X + 2 * M * C
 
 
@@ -31,31 +33,38 @@ def tile_attend_gedgew_kernel(tc, W, hT, dyT, soffs, toffs, out):
 
         toffs_t = held.tile([P, C // 16], U16, name="toffs_t")
         soffs_t = held.tile([P, C // 16], U16, name="soffs_t")
-        dy = [held.tile([P, X + PAD], F32, name="dy%d" % b) for b in range(BLOCKS)]
-        u = [held.tile([P, X + PAD], F32, name="u%d" % b) for b in range(BLOCKS)]
-        h_raw = [held.tile([P, PACK, HALF], F32, name="h_raw%d" % i, tag="h_raw%d" % i, align_bytes=64) for i in range(2)]
-        w_raw = [held.tile([P, PACK, HALF], F32, name="w_raw%d" % i, tag="w_raw%d" % i, align_bytes=64) for i in range(2)]
+        dy = held.tile([P, (BLOCKS - 2) * X + DY_WINDOW], F32, name="dy")
+        dy_at = [(BLOCKS - 1 - b) * X for b in range(BLOCKS)]
+        u = [held.tile([P, U_WINDOW], F32, name="u%d" % b) for b in range(BLOCKS)]
+        h_raw = [held.tile([P, PACK, HALF], F32, name="h_raw%d" % i) for i in range(2)]
+        w_raw = [held.tile([P, PACK, HALF], F32, name="w_raw%d" % i, tag="w_raw%d" % i) for i in range(2)]
         h_rows = hT.rearrange("(p j) x -> p j x", j=PACK)
         w_rows = W.rearrange("(p j) m -> p j m", j=PACK)
 
-        nc.sync.dma_start(dy[0][:, 0:X], dyT[0:P, :])
+        def load_dy(b):
+            nc.sync.dma_start(dy[:, dy_at[b] : dy_at[b] + X], dyT[b * P : (b + 1) * P, :])
+
+        def load_half(raw, rows, i):
+            nc.sync.dma_start(raw[i][:], rows[:, :, i * HALF : (i + 1) * HALF])
+
+        load_dy(0)
         nc.sync.dma_start(toffs_t[:], toffs)
-        nc.sync.dma_start(h_raw[0][:], h_rows[:, :, 0:HALF])
-        nc.sync.dma_start(dy[1][:, 0:X], dyT[P : 2 * P, :])
-        nc.sync.dma_start(h_raw[1][:], h_rows[:, :, HALF : 2 * HALF])
-        nc.sync.dma_start(dy[2][:, 0:X], dyT[2 * P : 3 * P, :])
-        nc.sync.dma_start(w_raw[0][:], w_rows[:, :, 0:HALF])
-        nc.sync.dma_start(w_raw[1][:], w_rows[:, :, HALF : 2 * HALF])
-        nc.sync.dma_start(dy[3][:, 0:X], dyT[3 * P : 4 * P, :])
+        load_dy(1)
+        load_half(h_raw, h_rows, 0)
+        load_dy(2)
+        load_half(h_raw, h_rows, 1)
+        load_half(w_raw, w_rows, 0)
+        load_dy(3)
+        load_half(w_raw, w_rows, 1)
         nc.sync.dma_start(soffs_t[:], soffs)
 
-        for b in range(BLOCKS):
-            nc.vector.memset(dy[b][:, X : X + PAD], 0.0)
-        for b in range(BLOCKS):
-            nc.vector.memset(u[b][:, X : X + PAD], 0.0)
+        nc.vector.memset(dy[:, BLOCKS * X :], 0.0)
         ident = held.tile([P, P], F32, name="ident")
         make_identity(nc, ident[:])
-        sums = held.tile([P, P], F32, name="sums")
+        for b in range(BLOCKS):
+            engine = nc.vector if b < 2 else nc.gpsimd
+            engine.memset(u[b][:, X:], 0.0)
+        sums = held.tile([P, 32], F32, name="sums", align_bytes=64)
         nc.gpsimd.memset(sums[:], 0.0)
 
         h_codes = held.tile([P, X], U32, name="h_codes", align_bytes=64)
@@ -63,8 +72,8 @@ def tile_attend_gedgew_kernel(tc, W, hT, dyT, soffs, toffs, out):
         w_codes = held.tile([P, M], U32, name="w_codes", align_bytes=64)
         w_scales = held.tile([P, M], U8, name="w_scales", align_bytes=64)
 
-        def quantise(raw, tag, codes, scales):
-            grouped = held.tile([P, HALF, PACK], BF16, name=tag, tag=tag, align_bytes=64)
+        def quantise(raw, name, codes, scales):
+            grouped = held.tile([P, HALF, PACK], BF16, name=name, align_bytes=64)
             nc.scalar.copy(
                 out=grouped[:].rearrange("p (c i) t -> p c t i", i=4),
                 in_=raw[:].rearrange("p t (c i) -> p c t i", i=4),
@@ -73,73 +82,65 @@ def tile_attend_gedgew_kernel(tc, W, hT, dyT, soffs, toffs, out):
                 out=codes.bitcast(FP8X4), scales=scales, in_=grouped[:].rearrange("p w j -> p (w j)")
             )
 
-        def gather_dy(b, e, tag):
-            g = held.tile([P, EDGES], F32, name="dg%d_%d" % (b, e), tag=tag, align_bytes=64)
-            cols = slice(e * EDGES // 16, (e + 1) * EDGES // 16)
-            nc.vector.tensor_copy(g[:], dy[b][:].indirect(toffs_t[:, cols]))
+        def gather_dy(b, tag):
+            g = held.tile([P, C], F32, name="dg%d" % b, tag=tag)
+            window = dy[:, dy_at[b] : dy_at[b] + DY_WINDOW] if b > 0 else dy[:, dy_at[b] :]
+            n = C if b > 0 else C // 2
+            for lo in range(0, C, n):
+                nc.vector.tensor_copy(g[:, lo : lo + n], window.indirect(toffs_t[:, lo // 16 : (lo + n) // 16]))
             return g
 
-        dg = {}
-        for b in range(2):
-            for e in range(2):
-                dg[b, e] = gather_dy(b, e, "dg%d_%d" % (b, e))
+        dg = [gather_dy(b, "dg%d" % b) for b in range(BLOCKS - 1)]
         for i in range(2):
             cols = slice(i * HALF, (i + 1) * HALF)
             quantise(h_raw[i], "hb%d" % i, h_codes[:, cols], h_scales[:, cols])
-            dg[2, i] = gather_dy(2, i, "h_raw%d" % i)
         for i in range(2):
             cols = slice(i * HALF, (i + 1) * HALF)
             quantise(w_raw[i], "wb%d" % i, w_codes[:, cols], w_scales[:, cols])
-            for b in (2 * i, 2 * i + 1):
-                acc = psum.tile([P, X], F32, name="acc%d" % b, tag="bank%d" % b)
-                mc = slice(b * P, (b + 1) * P)
-                nc.tensor.matmul_mx(
-                    out=acc[:],
-                    lhsT=w_codes[:, mc].bitcast(FP8X4),
-                    lhsT_scale=w_scales[:, mc],
-                    rhs=h_codes[:].bitcast(FP8X4),
-                    rhs_scale=h_scales[:],
-                    start=True,
-                    stop=True,
-                )
-                nc.scalar.copy(out=u[b][:, 0:X], in_=acc[:])
-            dg[3, i] = gather_dy(3, i, "w_raw%d" % i)
+            if i == 0:
+                dg.append(gather_dy(BLOCKS - 1, "w_raw0"))
+        for b in range(BLOCKS):
+            acc = psum.tile([P, X], F32, name="acc%d" % b, tag="bank%d" % b)
+            mc = slice(b * P, (b + 1) * P)
+            nc.tensor.matmul_mx(
+                out=acc[:],
+                lhsT=w_codes[:, mc].bitcast(FP8X4),
+                lhsT_scale=w_scales[:, mc],
+                rhs=h_codes[:].bitcast(FP8X4),
+                rhs_scale=h_scales[:],
+                start=True,
+                stop=True,
+            )
+            nc.scalar.copy(out=u[b][:, 0:X], in_=acc[:])
 
         junk = held.tile([P, P], F32, name="junk")
-        groups = EDGES // P
-        for e in range(2):
-            turned = [
-                psum.tile([P, P], F32, name="t%d_%d" % (e, g), tag="bank%d" % ((4 + 4 * e + g) % 8))
-                for g in range(groups)
-            ]
-            for b in range(BLOCKS):
-                last = e == 1 and b == BLOCKS - 1
-                pieces = [(0, 256), (256, 128), (384, 128)] if last else [(0, EDGES)]
-                for lo, n in pieces:
-                    q = held.tile([P, n], F32, name="q%d_%d_%d" % (e, b, lo))
-                    c0 = (e * EDGES + lo) // 16
-                    nc.vector.tensor_tensor(
-                        q[:], u[b][:].indirect(soffs_t[:, c0 : c0 + n // 16]), dg[b, e][:, lo : lo + n], mult
-                    )
-                    for k in range(n // P):
-                        g = lo // P + k
-                        nc.tensor.matmul(
-                            turned[g][:],
-                            q[:, k * P : (k + 1) * P],
-                            ident[:],
-                            start=(b == 0),
-                            stop=(b == BLOCKS - 1),
-                            is_transpose=True,
-                        )
-                        if b == BLOCKS - 1:
-                            col = sums[:, e * groups + g : e * groups + g + 1]
-                            if e == 1 and g == groups - 1:
-                                nc.vector.tensor_reduce(col, turned[g][:], mybir.AxisListType.X, add)
-                            else:
-                                nc.scalar.activation(junk[:], turned[g][:], copy, accum_out=col)
+        turned = [
+            psum.tile([P, P], F32, name="t%d" % g, tag="bank%d" % ((BLOCKS + g) % GROUPS)) for g in range(GROUPS)
+        ]
+        for b, lo, n in STEPS:
+            last = b == BLOCKS - 1
+            q = held.tile([P, n], F32, name="q%d_%d" % (b, lo))
+            nc.vector.tensor_tensor(
+                q[:], u[b][:].indirect(soffs_t[:, lo // 16 : (lo + n) // 16]), dg[b][:, lo : lo + n], mult
+            )
+            for k in range(n // P):
+                g = lo // P + k
+                nc.tensor.matmul(
+                    turned[g][:],
+                    q[:, k * P : (k + 1) * P],
+                    ident[:],
+                    start=(b == 0),
+                    stop=last,
+                    is_transpose=True,
+                )
+                if last and g >= 6:
+                    nc.vector.tensor_reduce(sums[:, g : g + 1], turned[g][:], mybir.AxisListType.X, add)
+                elif last:
+                    nc.scalar.activation(junk[:], turned[g][:], copy, accum_out=sums[:, g : g + 1])
 
-        rows = psum.tile([P, P], F32, name="rows", tag="bank4")
-        nc.tensor.transpose(rows[:], sums[:], ident[:])
-        res = held.tile([C // P, P], F32, name="res")
-        nc.vector.tensor_copy(res[:], rows[0 : C // P, :])
-        nc.sync.dma_start(out.rearrange("o (g p) -> (o g) p", p=P), res[:])
+        res = held.tile([P, 32], F32, name="res", align_bytes=64)
+        nc.vector.transpose(res[:], sums[:])
+        out_rows = out.rearrange("o (g q j) -> q (o g) j", q=4, j=32)
+        for quad in range(4):
+            queue = nc.sync if quad % 2 == 0 else nc.scalar
+            queue.dma_start(out_rows[quad], res[32 * quad : 32 * quad + GROUPS, :])

@@ -17,7 +17,7 @@ HALF = 256
 BLOCKS = M // P
 GROUPS = C // P
 DY_WINDOW = 1376
-U_WINDOW = C + 8
+U_WINDOW = [C + 8, C + 8, X + 8, X + 8]
 STEPS = [(0, 0, 1024), (1, 0, 1024), (2, 0, 512), (3, 0, 512), (2, 512, 512), (3, 512, 256), (3, 768, 128), (3, 896, 128)]
 FLOPS = 2 * D * M * X + 2 * M * C
 
@@ -33,9 +33,9 @@ def tile_attend_gedgew_kernel(tc, W, hT, dyT, soffs, toffs, out):
 
         toffs_t = held.tile([P, C // 16], U16, name="toffs_t")
         soffs_t = held.tile([P, C // 16], U16, name="soffs_t")
-        dy = held.tile([P, (BLOCKS - 2) * X + DY_WINDOW], F32, name="dy")
+        dy = held.tile([P, (BLOCKS - 1) * X + DY_WINDOW], F32, name="dy")
         dy_at = [(BLOCKS - 1 - b) * X for b in range(BLOCKS)]
-        u = [held.tile([P, U_WINDOW], F32, name="u%d" % b) for b in range(BLOCKS)]
+        u = [held.tile([P, U_WINDOW[b]], F32, name="u%d" % b) for b in range(BLOCKS)]
         h_raw = [held.tile([P, PACK, HALF], F32, name="h_raw%d" % i) for i in range(2)]
         w_raw = [held.tile([P, PACK, HALF], F32, name="w_raw%d" % i, tag="w_raw%d" % i) for i in range(2)]
         h_rows = hT.rearrange("(p j) x -> p j x", j=PACK)
@@ -62,8 +62,7 @@ def tile_attend_gedgew_kernel(tc, W, hT, dyT, soffs, toffs, out):
         ident = held.tile([P, P], F32, name="ident")
         make_identity(nc, ident[:])
         for b in range(BLOCKS):
-            engine = nc.vector if b < 2 else nc.gpsimd
-            engine.memset(u[b][:, X:], 0.0)
+            nc.vector.memset(u[b][:, X:], 0.0)
         sums = held.tile([P, 32], F32, name="sums", align_bytes=64)
         nc.gpsimd.memset(sums[:], 0.0)
 
@@ -72,31 +71,30 @@ def tile_attend_gedgew_kernel(tc, W, hT, dyT, soffs, toffs, out):
         w_codes = held.tile([P, M], U32, name="w_codes", align_bytes=64)
         w_scales = held.tile([P, M], U8, name="w_scales", align_bytes=64)
 
-        def quantise(raw, name, codes, scales):
-            grouped = held.tile([P, HALF, PACK], BF16, name=name, align_bytes=64)
+        def interleave(raw, grouped):
             nc.scalar.copy(
-                out=grouped[:].rearrange("p (c i) t -> p c t i", i=4),
+                out=grouped.rearrange("p (c i) t -> p c t i", i=4),
                 in_=raw[:].rearrange("p t (c i) -> p c t i", i=4),
             )
-            nc.vector.quantize_mx(
-                out=codes.bitcast(FP8X4), scales=scales, in_=grouped[:].rearrange("p w j -> p (w j)")
-            )
+
+        def quantise(grouped, codes, scales):
+            nc.vector.quantize_mx(out=codes.bitcast(FP8X4), scales=scales, in_=grouped.rearrange("p w j -> p (w j)"))
 
         def gather_dy(b, tag):
             g = held.tile([P, C], F32, name="dg%d" % b, tag=tag)
-            window = dy[:, dy_at[b] : dy_at[b] + DY_WINDOW] if b > 0 else dy[:, dy_at[b] :]
-            n = C if b > 0 else C // 2
-            for lo in range(0, C, n):
-                nc.vector.tensor_copy(g[:, lo : lo + n], window.indirect(toffs_t[:, lo // 16 : (lo + n) // 16]))
+            nc.vector.tensor_copy(g[:], dy[:, dy_at[b] : dy_at[b] + DY_WINDOW].indirect(toffs_t[:]))
             return g
 
         dg = [gather_dy(b, "dg%d" % b) for b in range(BLOCKS - 1)]
+        h_grouped = held.tile([P, X, PACK], BF16, name="h_grouped", align_bytes=64)
+        for i in range(2):
+            interleave(h_raw[i], h_grouped[:, i * HALF : (i + 1) * HALF, :])
+        quantise(h_grouped[:], h_codes[:], h_scales[:])
         for i in range(2):
             cols = slice(i * HALF, (i + 1) * HALF)
-            quantise(h_raw[i], "hb%d" % i, h_codes[:, cols], h_scales[:, cols])
-        for i in range(2):
-            cols = slice(i * HALF, (i + 1) * HALF)
-            quantise(w_raw[i], "wb%d" % i, w_codes[:, cols], w_scales[:, cols])
+            w_grouped = held.tile([P, HALF, PACK], BF16, name="w_grouped%d" % i, align_bytes=64)
+            interleave(w_raw[i], w_grouped[:])
+            quantise(w_grouped[:], w_codes[:, cols], w_scales[:, cols])
             if i == 0:
                 dg.append(gather_dy(BLOCKS - 1, "w_raw0"))
         for b in range(BLOCKS):

@@ -58,11 +58,8 @@ def tile_attend_gedgew_kernel(tc, W, hT, dyT, soffs, toffs, out):
         load_half(w_raw, w_rows, 1)
         nc.sync.dma_start(soffs_t[:], soffs)
 
-        nc.vector.memset(dy[:, BLOCKS * X :], 0.0)
         ident = held.tile([P, P], F32, name="ident")
         make_identity(nc, ident[:])
-        for b in range(BLOCKS):
-            nc.vector.memset(u[b][:, X:], 0.0)
         sums = held.tile([P, 32], F32, name="sums", align_bytes=64)
         nc.gpsimd.memset(sums[:], 0.0)
 

@@ -18,6 +18,8 @@ BLOCKS = M // P
 GROUPS = C // P
 DY_WINDOW = 1376
 U_WINDOW = [C + 8, C + 8, X + 8, X + 8]
+SQ = 32
+EARLY = 4
 STEPS = [(0, 0, 1024), (1, 0, 1024), (2, 0, 512), (3, 0, 512), (2, 512, 512), (3, 512, 256), (3, 768, 128), (3, 896, 128)]
 FLOPS = 2 * D * M * X + 2 * M * C
 
@@ -60,8 +62,10 @@ def tile_attend_gedgew_kernel(tc, W, hT, dyT, soffs, toffs, out):
 
         ident = held.tile([P, P], F32, name="ident")
         make_identity(nc, ident[:])
-        sums = held.tile([P, 32], F32, name="sums", align_bytes=64)
-        nc.gpsimd.memset(sums[:], 0.0)
+        early = held.tile([P, P], F32, name="early", align_bytes=64)
+        nc.gpsimd.memset(early[:], 0.0)
+        late = held.tile([P, P], F32, name="late", align_bytes=64)
+        nc.gpsimd.memset(late[:], 0.0)
 
         h_codes = held.tile([P, X], U32, name="h_codes", align_bytes=64)
         h_scales = held.tile([P, X], U8, name="h_scales", align_bytes=64)
@@ -128,14 +132,23 @@ def tile_attend_gedgew_kernel(tc, W, hT, dyT, soffs, toffs, out):
                     stop=last,
                     is_transpose=True,
                 )
-                if last and g >= 6:
-                    nc.vector.tensor_reduce(sums[:, g : g + 1], turned[g][:], mybir.AxisListType.X, add)
-                elif last:
-                    nc.scalar.activation(junk[:], turned[g][:], copy, accum_out=sums[:, g : g + 1])
+                if not last:
+                    continue
+                column = early[:, g : g + 1] if g < EARLY else late[:, SQ * (g - EARLY) : SQ * (g - EARLY) + 1]
+                if g >= 6:
+                    nc.vector.tensor_reduce(column, turned[g][:], mybir.AxisListType.X, add)
+                else:
+                    nc.scalar.activation(junk[:], turned[g][:], copy, accum_out=column)
+                if g == EARLY - 1:
+                    rows = psum.tile([P, P], F32, name="rows", tag="bank%d" % BLOCKS)
+                    nc.tensor.transpose(rows[:], early[:], ident[:])
+                    early_rows = held.tile([16, P], F32, name="early_rows")
+                    nc.scalar.copy(out=early_rows[:], in_=rows[0:16, :])
+                    nc.sync.dma_start(
+                        out.rearrange("o (g c) -> (o g) c", c=P)[0:EARLY, :], early_rows[0:EARLY, :]
+                    )
 
-        res = held.tile([P, 32], F32, name="res", align_bytes=64)
-        nc.vector.transpose(res[:], sums[:])
-        out_rows = out.rearrange("o (g q j) -> q (o g) j", q=4, j=32)
-        for quad in range(4):
-            queue = nc.sync if quad % 2 == 0 else nc.scalar
-            queue.dma_start(out_rows[quad], res[32 * quad : 32 * quad + GROUPS, :])
+        res = held.tile([P, P], F32, name="res", align_bytes=64)
+        out_rows = out.rearrange("o (g q j) -> (o q) g j", q=4, j=SQ)
+        nc.vector.transpose(res[:], late[:])
+        nc.sync.dma_start(out_rows[:, EARLY:GROUPS, :], res[0:P:SQ, :].rearrange("q (g j) -> q g j", j=SQ))

@@ -18,8 +18,6 @@ BLOCKS = M // P
 GROUPS = C // P
 DY_WINDOW = 1376
 U_WINDOW = [C + 8, C + 8, X + 8, X + 8]
-SQ = 32
-EARLY = 4
 STEPS = [(0, 0, 1024), (1, 0, 1024), (2, 0, 512), (3, 0, 512), (2, 512, 512), (3, 512, 256), (3, 768, 128), (3, 896, 128)]
 FLOPS = 2 * D * M * X + 2 * M * C
 
@@ -35,37 +33,27 @@ def tile_attend_gedgew_kernel(tc, W, hT, dyT, soffs, toffs, out):
 
         toffs_t = held.tile([P, C // 16], U16, name="toffs_t")
         soffs_t = held.tile([P, C // 16], U16, name="soffs_t")
-        dy = held.tile([P, (BLOCKS - 1) * X + DY_WINDOW], F32, name="dy")
-        dy_at = [(BLOCKS - 1 - b) * X for b in range(BLOCKS)]
+        dy = [held.tile([P, n, DY_WINDOW], F32, name="dy%d" % n0) for n0, n in ((0, 1), (1, 1), (2, 2))]
+        dy_window = [dy[0][:, 0, :], dy[1][:, 0, :], dy[2][:, 0, :], dy[2][:, 1, :]]
         u = [held.tile([P, U_WINDOW[b]], F32, name="u%d" % b) for b in range(BLOCKS)]
-        h_raw = [held.tile([P, PACK, HALF], F32, name="h_raw%d" % i) for i in range(2)]
+        h_raw = held.tile([P, PACK, X], F32, name="h_raw")
         w_raw = [held.tile([P, PACK, HALF], F32, name="w_raw%d" % i, tag="w_raw%d" % i) for i in range(2)]
-        h_rows = hT.rearrange("(p j) x -> p j x", j=PACK)
         w_rows = W.rearrange("(p j) m -> p j m", j=PACK)
+        dy_rows = dyT.rearrange("(b p) x -> p b x", p=P)
 
-        def load_dy(b):
-            nc.sync.dma_start(dy[:, dy_at[b] : dy_at[b] + X], dyT[b * P : (b + 1) * P, :])
-
-        def load_half(raw, rows, i):
-            nc.sync.dma_start(raw[i][:], rows[:, :, i * HALF : (i + 1) * HALF])
-
-        load_dy(0)
         nc.sync.dma_start(toffs_t[:], toffs)
-        load_dy(1)
-        load_half(h_raw, h_rows, 0)
-        load_dy(2)
-        load_half(h_raw, h_rows, 1)
-        load_half(w_raw, w_rows, 0)
-        load_dy(3)
-        load_half(w_raw, w_rows, 1)
+        nc.scalar.dma_start(dy[0][:, :, 0:X], dy_rows[:, 0:1, :])
+        nc.scalar.dma_start(dy[1][:, :, 0:X], dy_rows[:, 1:2, :])
+        nc.scalar.dma_start(h_raw[:], hT.rearrange("(p j) x -> p j x", j=PACK))
+        nc.scalar.dma_start(dy[2][:, :, 0:X], dy_rows[:, 2:4, :])
+        for i in range(2):
+            nc.scalar.dma_start(w_raw[i][:], w_rows[:, :, i * HALF : (i + 1) * HALF])
         nc.sync.dma_start(soffs_t[:], soffs)
 
         ident = held.tile([P, P], F32, name="ident")
         make_identity(nc, ident[:])
-        early = held.tile([P, P], F32, name="early", align_bytes=64)
-        nc.gpsimd.memset(early[:], 0.0)
-        late = held.tile([P, P], F32, name="late", align_bytes=64)
-        nc.gpsimd.memset(late[:], 0.0)
+        sums = held.tile([P, 32], F32, name="sums", align_bytes=64)
+        nc.gpsimd.memset(sums[:], 0.0)
 
         h_codes = held.tile([P, X], U32, name="h_codes", align_bytes=64)
         h_scales = held.tile([P, X], U8, name="h_scales", align_bytes=64)
@@ -75,7 +63,7 @@ def tile_attend_gedgew_kernel(tc, W, hT, dyT, soffs, toffs, out):
         def interleave(raw, grouped):
             nc.scalar.copy(
                 out=grouped.rearrange("p (c i) t -> p c t i", i=4),
-                in_=raw[:].rearrange("p t (c i) -> p c t i", i=4),
+                in_=raw.rearrange("p t (c i) -> p c t i", i=4),
             )
 
         def quantise(grouped, codes, scales):
@@ -83,18 +71,17 @@ def tile_attend_gedgew_kernel(tc, W, hT, dyT, soffs, toffs, out):
 
         def gather_dy(b, tag):
             g = held.tile([P, C], F32, name="dg%d" % b, tag=tag)
-            nc.vector.tensor_copy(g[:], dy[:, dy_at[b] : dy_at[b] + DY_WINDOW].indirect(toffs_t[:]))
+            nc.vector.tensor_copy(g[:], dy_window[b].indirect(toffs_t[:]))
             return g
 
         dg = [gather_dy(b, "dg%d" % b) for b in range(BLOCKS - 1)]
         h_grouped = held.tile([P, X, PACK], BF16, name="h_grouped", align_bytes=64)
-        for i in range(2):
-            interleave(h_raw[i], h_grouped[:, i * HALF : (i + 1) * HALF, :])
+        interleave(h_raw[:], h_grouped[:])
         quantise(h_grouped[:], h_codes[:], h_scales[:])
         for i in range(2):
             cols = slice(i * HALF, (i + 1) * HALF)
             w_grouped = held.tile([P, HALF, PACK], BF16, name="w_grouped%d" % i, align_bytes=64)
-            interleave(w_raw[i], w_grouped[:])
+            interleave(w_raw[i][:], w_grouped[:])
             quantise(w_grouped[:], w_codes[:, cols], w_scales[:, cols])
             if i == 0:
                 dg.append(gather_dy(BLOCKS - 1, "w_raw0"))
@@ -132,23 +119,14 @@ def tile_attend_gedgew_kernel(tc, W, hT, dyT, soffs, toffs, out):
                     stop=last,
                     is_transpose=True,
                 )
-                if not last:
-                    continue
-                column = early[:, g : g + 1] if g < EARLY else late[:, SQ * (g - EARLY) : SQ * (g - EARLY) + 1]
-                if g >= 6:
-                    nc.vector.tensor_reduce(column, turned[g][:], mybir.AxisListType.X, add)
-                else:
-                    nc.scalar.activation(junk[:], turned[g][:], copy, accum_out=column)
-                if g == EARLY - 1:
-                    rows = psum.tile([P, P], F32, name="rows", tag="bank%d" % BLOCKS)
-                    nc.tensor.transpose(rows[:], early[:], ident[:])
-                    early_rows = held.tile([16, P], F32, name="early_rows")
-                    nc.scalar.copy(out=early_rows[:], in_=rows[0:16, :])
-                    nc.sync.dma_start(
-                        out.rearrange("o (g c) -> (o g) c", c=P)[0:EARLY, :], early_rows[0:EARLY, :]
-                    )
+                if last and g >= 6:
+                    nc.vector.tensor_reduce(sums[:, g : g + 1], turned[g][:], mybir.AxisListType.X, add)
+                elif last:
+                    nc.scalar.activation(junk[:], turned[g][:], copy, accum_out=sums[:, g : g + 1])
 
-        res = held.tile([P, P], F32, name="res", align_bytes=64)
-        out_rows = out.rearrange("o (g q j) -> (o q) g j", q=4, j=SQ)
-        nc.vector.transpose(res[:], late[:])
-        nc.sync.dma_start(out_rows[:, EARLY:GROUPS, :], res[0:P:SQ, :].rearrange("q (g j) -> q g j", j=SQ))
+        res = held.tile([P, 32], F32, name="res", align_bytes=64)
+        nc.vector.transpose(res[:], sums[:])
+        out_rows = out.rearrange("o (g q j) -> q (o g) j", q=4, j=32)
+        for quad in range(4):
+            queue = nc.sync if quad % 2 == 0 else nc.scalar
+            queue.dma_start(out_rows[quad], res[32 * quad : 32 * quad + GROUPS, :])

@@ -18,6 +18,8 @@ BLOCKS = M // P
 GROUPS = C // P
 DY_WINDOW = 1376
 U_WINDOW = [C + 8, C + 8, X + 8, X + 8]
+SQ = 32
+EARLY = 6
 STEPS = [(0, 0, 1024), (1, 0, 1024), (2, 0, 512), (3, 0, 512), (2, 512, 512), (3, 512, 256), (3, 768, 128), (3, 896, 128)]
 FLOPS = 2 * D * M * X + 2 * M * C
 
@@ -52,8 +54,9 @@ def tile_attend_gedgew_kernel(tc, W, hT, dyT, soffs, toffs, out):
 
         ident = held.tile([P, P], F32, name="ident")
         make_identity(nc, ident[:])
-        sums = held.tile([P, 32], F32, name="sums", align_bytes=64)
-        nc.gpsimd.memset(sums[:], 0.0)
+        sums = [held.tile([P, SQ], F32, name="sums%d" % i, align_bytes=64) for i in range(2)]
+        for i in range(2):
+            nc.gpsimd.memset(sums[i][:], 0.0)
 
         h_codes = held.tile([P, X], U32, name="h_codes", align_bytes=64)
         h_scales = held.tile([P, X], U8, name="h_scales", align_bytes=64)
@@ -99,10 +102,10 @@ def tile_attend_gedgew_kernel(tc, W, hT, dyT, soffs, toffs, out):
             )
             nc.scalar.copy(out=u[b][:, 0:X], in_=acc[:])
 
-        junk = held.tile([P, P], F32, name="junk")
         turned = [
             psum.tile([P, P], F32, name="t%d" % g, tag="bank%d" % ((BLOCKS + g) % GROUPS)) for g in range(GROUPS)
         ]
+        out_rows = out.rearrange("o (g q j) -> (o g) q j", q=4, j=SQ)
         for b, lo, n in STEPS:
             last = b == BLOCKS - 1
             q = held.tile([P, n], F32, name="q%d_%d" % (b, lo))
@@ -119,14 +122,17 @@ def tile_attend_gedgew_kernel(tc, W, hT, dyT, soffs, toffs, out):
                     stop=last,
                     is_transpose=True,
                 )
-                if last and g >= 6:
-                    nc.vector.tensor_reduce(sums[:, g : g + 1], turned[g][:], mybir.AxisListType.X, add)
-                elif last:
-                    nc.scalar.activation(junk[:], turned[g][:], copy, accum_out=sums[:, g : g + 1])
-
-        res = held.tile([P, 32], F32, name="res", align_bytes=64)
-        nc.vector.transpose(res[:], sums[:])
-        out_rows = out.rearrange("o (g q j) -> q (o g) j", q=4, j=32)
-        for quad in range(4):
-            queue = nc.sync if quad % 2 == 0 else nc.scalar
-            queue.dma_start(out_rows[quad], res[32 * quad : 32 * quad + GROUPS, :])
+                if not last:
+                    continue
+                column = sums[g // EARLY][:, g : g + 1]
+                if g == GROUPS - 1:
+                    nc.vector.tensor_reduce(column, turned[g][:], mybir.AxisListType.X, add)
+                else:
+                    junk = held.tile([P, P], F32, name="junk%d" % g)
+                    nc.scalar.activation(junk[:], turned[g][:], copy, accum_out=column)
+                if g in (EARLY - 1, GROUPS - 1):
+                    res = held.tile([P, SQ], F32, name="res%d" % g, align_bytes=64)
+                    nc.vector.transpose(res[:], sums[g // EARLY][:])
+                    for r in range(0 if g < EARLY else EARLY, g + 1):
+                        queue = nc.sync if r % 2 == 1 else nc.scalar
+                        queue.dma_start(out_rows[r], res[r:P:SQ, :])

@@ -19,7 +19,7 @@ GROUPS = C // P
 DY_WINDOW = 1376
 U_WINDOW = [C + 8, C + 8, X + 8, X + 8]
 SQ = 32
-EARLY = 6
+SETS = [range(0, 4), range(4, 6), range(6, 7), range(7, 8)]
 STEPS = [(0, 0, 1024), (1, 0, 1024), (2, 0, 512), (3, 0, 512), (2, 512, 512), (3, 512, 256), (3, 768, 128), (3, 896, 128)]
 FLOPS = 2 * D * M * X + 2 * M * C
 
@@ -54,8 +54,8 @@ def tile_attend_gedgew_kernel(tc, W, hT, dyT, soffs, toffs, out):
 
         ident = held.tile([P, P], F32, name="ident")
         make_identity(nc, ident[:])
-        sums = [held.tile([P, SQ], F32, name="sums%d" % i, align_bytes=64) for i in range(2)]
-        for i in range(2):
+        sums = [held.tile([P, SQ], F32, name="sums%d" % i, align_bytes=64) for i in range(len(SETS))]
+        for i in range(len(SETS)):
             nc.gpsimd.memset(sums[i][:], 0.0)
 
         h_codes = held.tile([P, X], U32, name="h_codes", align_bytes=64)
@@ -124,15 +124,17 @@ def tile_attend_gedgew_kernel(tc, W, hT, dyT, soffs, toffs, out):
                 )
                 if not last:
                     continue
-                column = sums[g // EARLY][:, g : g + 1]
+                which = [g in members for members in SETS].index(True)
+                held_in = sums[which]
+                column = held_in[:, g : g + 1]
                 if g == GROUPS - 1:
                     nc.vector.tensor_reduce(column, turned[g][:], mybir.AxisListType.X, add)
                 else:
                     junk = held.tile([P, P], F32, name="junk%d" % g)
                     nc.scalar.activation(junk[:], turned[g][:], copy, accum_out=column)
-                if g in (EARLY - 1, GROUPS - 1):
+                if g == SETS[which][-1]:
                     res = held.tile([P, SQ], F32, name="res%d" % g, align_bytes=64)
-                    nc.vector.transpose(res[:], sums[g // EARLY][:])
-                    for r in range(0 if g < EARLY else EARLY, g + 1):
-                        queue = nc.sync if r % 2 == 1 else nc.scalar
+                    nc.vector.transpose(res[:], held_in[:])
+                    for r in SETS[which]:
+                        queue = nc.scalar if r == GROUPS - 2 else nc.sync
                         queue.dma_start(out_rows[r], res[r:P:SQ, :])

@@ -17,10 +17,10 @@ HALF = 256
 BLOCKS = M // P
 GROUPS = C // P
 DY_WINDOW = 1376
-U_WINDOW = [C + 8, C + 8, X + 8, X + 8]
+U_WINDOW = [C + 8, C + 8, 776, X + 8]
 SQ = 32
-SETS = [range(0, 4), range(4, 6), range(6, 7), range(7, 8)]
-STEPS = [(0, 0, 1024), (1, 0, 1024), (2, 0, 512), (3, 0, 512), (2, 512, 512), (3, 512, 256), (3, 768, 128), (3, 896, 128)]
+SETS = [range(0, 6), range(6, 7), range(7, 8)]
+STEPS = [(0, 0, 1024), (1, 0, 1024), (2, 0, 768), (3, 0, 512), (3, 512, 256), (2, 768, 256), (3, 768, 128), (3, 896, 128)]
 FLOPS = 2 * D * M * X + 2 * M * C
 
 
@@ -54,8 +54,8 @@ def tile_attend_gedgew_kernel(tc, W, hT, dyT, soffs, toffs, out):
 
         ident = held.tile([P, P], F32, name="ident")
         make_identity(nc, ident[:])
-        sums = [held.tile([P, SQ], F32, name="sums%d" % i, align_bytes=64) for i in range(len(SETS))]
-        for i in range(len(SETS)):
+        sums = [held.tile([P, SQ], F32, name="sums%d" % i, align_bytes=64) for i in range(2)]
+        for i in range(2):
             nc.gpsimd.memset(sums[i][:], 0.0)
 
         h_codes = held.tile([P, X], U32, name="h_codes", align_bytes=64)
@@ -125,7 +125,7 @@ def tile_attend_gedgew_kernel(tc, W, hT, dyT, soffs, toffs, out):
                 if not last:
                     continue
                 which = [g in members for members in SETS].index(True)
-                held_in = sums[which]
+                held_in = sums[which % 2]
                 column = held_in[:, g : g + 1]
                 if g == GROUPS - 1:
                     nc.vector.tensor_reduce(column, turned[g][:], mybir.AxisListType.X, add)

@@ -20,6 +20,9 @@ DY_WINDOW = 1376
 U_WINDOW = [C + 8, C + 8, 776, X + 8]
 SQ = 32
 SETS = [range(0, 6), range(6, 7), range(7, 8)]
+TURN_AT = [16, 0, 32]
+SUM_AT = [16, 17, 18, 19, 20, 21, 24, 40]
+ON_SCALAR_QUEUE = (4, 5, 6)
 STEPS = [(0, 0, 1024), (1, 0, 1024), (2, 0, 768), (3, 0, 512), (3, 512, 256), (2, 768, 256), (3, 768, 128), (3, 896, 128)]
 FLOPS = 2 * D * M * X + 2 * M * C
 
@@ -54,9 +57,8 @@ def tile_attend_gedgew_kernel(tc, W, hT, dyT, soffs, toffs, out):
 
         ident = held.tile([P, P], F32, name="ident")
         make_identity(nc, ident[:])
-        sums = [held.tile([P, SQ], F32, name="sums%d" % i, align_bytes=64) for i in range(2)]
-        for i in range(2):
-            nc.gpsimd.memset(sums[i][:], 0.0)
+        sums = held.tile([P, 2 * SQ], F32, name="sums", align_bytes=64)
+        nc.gpsimd.memset(sums[:], 0.0)
 
         h_codes = held.tile([P, X], U32, name="h_codes", align_bytes=64)
         h_scales = held.tile([P, X], U8, name="h_scales", align_bytes=64)
@@ -125,16 +127,15 @@ def tile_attend_gedgew_kernel(tc, W, hT, dyT, soffs, toffs, out):
                 if not last:
                     continue
                 which = [g in members for members in SETS].index(True)
-                held_in = sums[which % 2]
-                column = held_in[:, g : g + 1]
-                if g == GROUPS - 1:
+                column = sums[:, SUM_AT[g] : SUM_AT[g] + 1]
+                if which > 0:
                     nc.vector.tensor_reduce(column, turned[g][:], mybir.AxisListType.X, add)
                 else:
                     junk = held.tile([P, P], F32, name="junk%d" % g)
                     nc.scalar.activation(junk[:], turned[g][:], copy, accum_out=column)
                 if g == SETS[which][-1]:
                     res = held.tile([P, SQ], F32, name="res%d" % g, align_bytes=64)
-                    nc.vector.transpose(res[:], held_in[:])
+                    nc.vector.transpose(res[:], sums[:, TURN_AT[which] : TURN_AT[which] + SQ])
                     for r in SETS[which]:
-                        queue = nc.scalar if r == GROUPS - 2 else nc.sync
-                        queue.dma_start(out_rows[r], res[r:P:SQ, :])
+                        queue = nc.scalar if r in ON_SCALAR_QUEUE else nc.sync
+                        queue.dma_start(out_rows[r], res[SUM_AT[r] - TURN_AT[which] : P : SQ, :])

@@ -15,15 +15,11 @@ PACK = 4
 D, M, X, C = 512, 512, 512, 1024
 HALF = 256
 BLOCKS = M // P
-GROUPS = C // P
-DY_WINDOW = 1376
-U_WINDOW = [C + 8, C + 8, 776, X + 8]
+WINDOW = C + 8
+SHARE = 704
 SQ = 32
-SETS = [range(0, 6), range(6, 7), range(7, 8)]
-TURN_AT = [16, 0, 32]
-SUM_AT = [16, 17, 18, 19, 20, 21, 24, 40]
-ON_SCALAR_QUEUE = (4, 5, 6)
-STEPS = [(0, 0, 1024), (1, 0, 1024), (2, 0, 768), (3, 0, 512), (3, 512, 256), (2, 768, 256), (3, 768, 128), (3, 896, 128)]
+MID = C // 2
+SETS = [range(0, 4), range(4, 6), range(6, 8)]
 FLOPS = 2 * D * M * X + 2 * M * C
 
 
@@ -38,104 +34,163 @@ def tile_attend_gedgew_kernel(tc, W, hT, dyT, soffs, toffs, out):
 
         toffs_t = held.tile([P, C // 16], U16, name="toffs_t")
         soffs_t = held.tile([P, C // 16], U16, name="soffs_t")
-        dy = [held.tile([P, n, DY_WINDOW], F32, name="dy%d" % n0) for n0, n in ((0, 1), (1, 1), (2, 2))]
-        dy_window = [dy[0][:, 0, :], dy[1][:, 0, :], dy[2][:, 0, :], dy[2][:, 1, :]]
-        u = [held.tile([P, U_WINDOW[b]], F32, name="u%d" % b) for b in range(BLOCKS)]
-        h_raw = held.tile([P, PACK, X], F32, name="h_raw")
-        w_raw = [held.tile([P, PACK, HALF], F32, name="w_raw%d" % i, tag="w_raw%d" % i) for i in range(2)]
+        dy = [held.tile([P, WINDOW], F32, name="dy%d" % b) for b in range(BLOCKS)]
+        u = [held.tile([P, WINDOW], F32, name="u%d" % b) for b in range(BLOCKS)]
+        h_raw = [
+            held.tile([P, PACK, HALF], F32, name="h_raw%d" % i, tag="h_raw%d" % i, align_bytes=64) for i in range(2)
+        ]
+        w_cols = [slice(0, P), slice(P, HALF), slice(HALF, M)]
+        w_raw = [
+            held.tile([P, PACK, c.stop - c.start], F32, name="w_raw%d" % i, tag="w_raw%d" % i, align_bytes=64)
+            for i, c in enumerate(w_cols)
+        ]
         w_rows = W.rearrange("(p j) m -> p j m", j=PACK)
-        dy_rows = dyT.rearrange("(b p) x -> p b x", p=P)
+        h_rows = hT.rearrange("(p j) x -> p j x", j=PACK)
+
+        def load_dy(b):
+            nc.sync.dma_start(dy[b][:, 0:X], dyT[b * P : (b + 1) * P, :])
 
         nc.sync.dma_start(toffs_t[:], toffs)
-        nc.scalar.dma_start(dy[0][:, :, 0:X], dy_rows[:, 0:1, :])
-        nc.scalar.dma_start(dy[1][:, :, 0:X], dy_rows[:, 1:2, :])
-        nc.scalar.dma_start(h_raw[:], hT.rearrange("(p j) x -> p j x", j=PACK))
-        nc.scalar.dma_start(dy[2][:, :, 0:X], dy_rows[:, 2:4, :])
-        for i in range(2):
-            nc.scalar.dma_start(w_raw[i][:], w_rows[:, :, i * HALF : (i + 1) * HALF])
+        load_dy(0)
+        load_dy(1)
+        nc.sync.dma_start(h_raw[0][:], h_rows[:, :, 0:HALF])
+        nc.sync.dma_start(w_raw[0][:], w_rows[:, :, w_cols[0]])
+        nc.sync.dma_start(h_raw[1][:], h_rows[:, :, HALF:X])
+        nc.sync.dma_start(w_raw[1][:], w_rows[:, :, w_cols[1]])
+        nc.sync.dma_start(w_raw[2][:], w_rows[:, :, w_cols[2]])
         nc.sync.dma_start(soffs_t[:], soffs)
+        load_dy(2)
+        load_dy(3)
 
         ident = held.tile([P, P], F32, name="ident")
         make_identity(nc, ident[:])
-        sums = held.tile([P, 2 * SQ], F32, name="sums", align_bytes=64)
-        nc.gpsimd.memset(sums[:], 0.0)
+        sums = [held.tile([P, SQ], F32, name="sums%d" % i, align_bytes=64) for i in range(len(SETS))]
+        nc.vector.memset(sums[0][:], 0.0)
+        for later in sums[1:]:
+            nc.scalar.copy(later[:], sums[0][:])
 
-        h_codes = held.tile([P, X], U32, name="h_codes", align_bytes=64)
+        h_codes = held.tile([P, X], U32, name="h_codes", tag="h_codes", align_bytes=64)
         h_scales = held.tile([P, X], U8, name="h_scales", align_bytes=64)
-        w_codes = held.tile([P, M], U32, name="w_codes", align_bytes=64)
+        w_codes = held.tile([P, M], U32, name="w_codes", tag="w_codes", align_bytes=64)
         w_scales = held.tile([P, M], U8, name="w_scales", align_bytes=64)
 
-        def interleave(raw, grouped):
-            nc.scalar.copy(
+        def interleave(move, raw, grouped):
+            move(
                 out=grouped.rearrange("p (c i) t -> p c t i", i=4),
                 in_=raw.rearrange("p t (c i) -> p c t i", i=4),
             )
 
+        def grouped_tile(width, name, tag=None):
+            return held.tile([P, width, PACK], BF16, name=name, tag=tag or name, align_bytes=64)
+
         def quantise(grouped, codes, scales):
-            nc.vector.quantize_mx(out=codes.bitcast(FP8X4), scales=scales, in_=grouped.rearrange("p w j -> p (w j)"))
+            nc.vector.quantize_mx(
+                out=codes.bitcast(FP8X4), scales=scales, in_=grouped[:].rearrange("p w j -> p (w j)")
+            )
 
-        def gather_dy(b, tag):
-            g = held.tile([P, C], F32, name="dg%d" % b, tag=tag)
-            nc.vector.tensor_copy(g[:], dy_window[b].indirect(toffs_t[:]))
-            return g
-
-        dg = [gather_dy(b, "dg%d" % b) for b in range(BLOCKS - 1)]
-        h_grouped = held.tile([P, X, PACK], BF16, name="h_grouped", align_bytes=64)
-        interleave(h_raw[:], h_grouped[:])
-        quantise(h_grouped[:], h_codes[:], h_scales[:])
-        for i in range(2):
-            cols = slice(i * HALF, (i + 1) * HALF)
-            w_grouped = held.tile([P, HALF, PACK], BF16, name="w_grouped%d" % i, align_bytes=64)
-            interleave(w_raw[i][:], w_grouped[:])
-            quantise(w_grouped[:], w_codes[:, cols], w_scales[:, cols])
-            if i == 0:
-                dg.append(gather_dy(BLOCKS - 1, "w_raw0"))
-        for b in range(BLOCKS):
-            acc = psum.tile([P, X], F32, name="acc%d" % b, tag="bank%d" % b)
+        def multiply(b, lo, hi, bank):
+            acc = psum.tile([P, hi - lo], F32, name="acc%d_%d" % (b, lo), tag=bank)
             mc = slice(b * P, (b + 1) * P)
             nc.tensor.matmul_mx(
                 out=acc[:],
                 lhsT=w_codes[:, mc].bitcast(FP8X4),
                 lhsT_scale=w_scales[:, mc],
-                rhs=h_codes[:].bitcast(FP8X4),
-                rhs_scale=h_scales[:],
+                rhs=h_codes[:, lo:hi].bitcast(FP8X4),
+                rhs_scale=h_scales[:, lo:hi],
                 start=True,
                 stop=True,
             )
-            nc.scalar.copy(out=u[b][:, 0:X], in_=acc[:])
+            return acc
+
+        def edges(offsets, lo, hi):
+            return offsets[:, lo // 16 : hi // 16]
+
+        def scalar_gather(window, offsets, lo, hi, name, tag=None):
+            picked = held.tile([P, hi - lo], F32, name=name, tag=tag or name, align_bytes=64)
+            nc.scalar.activation(picked[:], window[:].indirect(edges(offsets, lo, hi)), copy)
+            return picked
+
+        dg0 = held.tile([P, C], F32, name="dg0")
+        nc.vector.tensor_copy(dg0[:, 0:SHARE], dy[0][:].indirect(edges(toffs_t, 0, SHARE)))
+        nc.scalar.activation(dg0[:, SHARE:C], dy[0][:].indirect(edges(toffs_t, SHARE, C)), copy)
+        dg1 = scalar_gather(dy[1], toffs_t, 0, C, "dg1")
+
+        h_grouped = [grouped_tile(HALF, "h_grouped%d" % i) for i in range(2)]
+        w_grouped = [grouped_tile(P, "w_grouped0")]
+        interleave(nc.vector.tensor_copy, h_raw[0][:], h_grouped[0][:])
+        interleave(nc.vector.tensor_copy, w_raw[0][:], w_grouped[0][:])
+        quantise(h_grouped[0], h_codes[:, 0:HALF], h_scales[:, 0:HALF])
+        quantise(w_grouped[0], w_codes[:, 0:P], w_scales[:, 0:P])
+        interleave(nc.vector.tensor_copy, h_raw[1][:, :, 0:P], h_grouped[1][:, 0:P, :])
+        interleave(nc.scalar.copy, h_raw[1][:, :, P:HALF], h_grouped[1][:, P:HALF, :])
+        quantise(h_grouped[1], h_codes[:, HALF:X], h_scales[:, HALF:X])
+        nc.scalar.copy(out=u[0][:, 0:HALF], in_=multiply(0, 0, HALF, "bank0")[:])
+        w_grouped.append(grouped_tile(P, "w_grouped1", "h_raw1"))
+        interleave(nc.scalar.copy, w_raw[1][:], w_grouped[1][:])
+        quantise(w_grouped[1], w_codes[:, P:HALF], w_scales[:, P:HALF])
+        nc.vector.tensor_copy(out=u[0][:, HALF:X], in_=multiply(0, HALF, X, "bank1")[:])
+        w_grouped.append(grouped_tile(HALF, "w_grouped2", "w_raw1"))
+        interleave(nc.scalar.copy, w_raw[2][:], w_grouped[2][:])
+        nc.scalar.copy(out=u[1][:, 0:X], in_=multiply(1, 0, X, "bank2")[:])
+        dg2 = scalar_gather(dy[2], toffs_t, 0, C, "dg2", tag="w_raw2")
 
         turned = [
-            psum.tile([P, P], F32, name="t%d" % g, tag="bank%d" % ((BLOCKS + g) % GROUPS)) for g in range(GROUPS)
+            psum.tile([P, len(members), P], F32, name="turned%d" % i, tag="bank%d" % (5 + i))
+            for i, members in enumerate(SETS)
         ]
         out_rows = out.rearrange("o (g q j) -> (o g) q j", q=4, j=SQ)
-        for b, lo, n in STEPS:
-            last = b == BLOCKS - 1
-            q = held.tile([P, n], F32, name="q%d_%d" % (b, lo))
-            nc.vector.tensor_tensor(
-                q[:], u[b][:].indirect(soffs_t[:, lo // 16 : (lo + n) // 16]), dg[b][:, lo : lo + n], mult
-            )
-            for k in range(n // P):
+
+        def add_up(q, b, lo, hi):
+            for k in range((hi - lo) // P):
                 g = lo // P + k
+                which = [g in members for members in SETS].index(True)
+                members = SETS[which]
+                closes = b == BLOCKS - 1 and g == members[-1]
                 nc.tensor.matmul(
-                    turned[g][:],
+                    turned[which][:, g - members[0], :],
                     q[:, k * P : (k + 1) * P],
                     ident[:],
-                    start=(b == 0),
-                    stop=last,
+                    start=(b == 0 and g == members[0]),
+                    stop=closes,
                     is_transpose=True,
                 )
-                if not last:
-                    continue
-                which = [g in members for members in SETS].index(True)
-                column = sums[:, SUM_AT[g] : SUM_AT[g] + 1]
-                if which > 0:
-                    nc.vector.tensor_reduce(column, turned[g][:], mybir.AxisListType.X, add)
-                else:
+                if closes:
+                    close(which)
+
+        def close(which):
+            members = SETS[which]
+            if which == len(SETS) - 1:
+                nc.vector.tensor_reduce(sums[which][:, 0 : len(members)], turned[which][:], mybir.AxisListType.X, add)
+            else:
+                for k, g in enumerate(members):
                     junk = held.tile([P, P], F32, name="junk%d" % g)
-                    nc.scalar.activation(junk[:], turned[g][:], copy, accum_out=column)
-                if g == SETS[which][-1]:
-                    res = held.tile([P, SQ], F32, name="res%d" % g, align_bytes=64)
-                    nc.vector.transpose(res[:], sums[:, TURN_AT[which] : TURN_AT[which] + SQ])
-                    for r in SETS[which]:
-                        queue = nc.scalar if r in ON_SCALAR_QUEUE else nc.sync
-                        queue.dma_start(out_rows[r], res[SUM_AT[r] - TURN_AT[which] : P : SQ, :])
+                    nc.scalar.activation(junk[:], turned[which][:, k, :], copy, accum_out=sums[which][:, k : k + 1])
+            res = held.tile([P, SQ], F32, name="res%d" % which, align_bytes=64)
+            nc.vector.transpose(res[:], sums[which][:])
+            for k, g in enumerate(members):
+                queue = nc.scalar if g == 6 else nc.sync
+                queue.dma_start(out_rows[g], res[k:P:SQ, :])
+
+        def fused(b, lo, hi, picked, tag=None):
+            name = "q%d_%d" % (b, lo)
+            q = held.tile([P, hi - lo], F32, name=name, tag=tag or name, align_bytes=64)
+            nc.vector.tensor_tensor(q[:], u[b][:].indirect(edges(soffs_t, lo, hi)), picked, mult)
+            add_up(q, b, lo, hi)
+
+        fused(0, 0, MID, dg0[:, 0:MID])
+        quantise(w_grouped[2], w_codes[:, HALF:M], w_scales[:, HALF:M])
+        fused(0, MID, C, dg0[:, MID:C], tag="w_raw1")
+        for b in (2, 3):
+            nc.scalar.copy(out=u[b][:, 0:X], in_=multiply(b, 0, X, "bank%d" % (b + 1))[:])
+        dg3a = scalar_gather(dy[3], toffs_t, 0, MID, "dg3a", tag="w_codes")
+        dg3b = scalar_gather(dy[3], toffs_t, MID, C, "dg3b", tag="h_codes")
+        ug3b = scalar_gather(u[3], soffs_t, MID, C, "ug3b")
+        fused(1, 0, C, dg1[:])
+        fused(2, 0, MID, dg2[:, 0:MID])
+        fused(3, 0, MID, dg3a[:])
+        fused(2, MID, C, dg2[:, MID:C])
+        for lo in (MID, MID + HALF):
+            q = held.tile([P, HALF], F32, name="q3_%d" % lo)
+            part = slice(lo - MID, lo - MID + HALF)
+            nc.vector.tensor_tensor(q[:], ug3b[:, part], dg3b[:, part], mult)
+            add_up(q, 3, lo, lo + HALF)

@@ -16,10 +16,14 @@ D, M, X, C = 512, 512, 512, 1024
 HALF = 256
 BLOCKS = M // P
 WINDOW = C + 8
-SHARE = 704
+WIDE_WINDOW = 1376
 SQ = 32
 MID = C // 2
-SETS = [range(0, 4), range(4, 6), range(6, 8)]
+BANKS = [range(g, g + 1) for g in range(8)]
+SETS = [range(0, 6), range(6, 7), range(7, 8)]
+TURN_AT = [16, 0, 32]
+SUM_AT = [16, 17, 18, 19, 20, 21, 24, 40]
+ON_SCALAR_QUEUE = (4, 5, 6)
 FLOPS = 2 * D * M * X + 2 * M * C
 
 
@@ -32,20 +36,16 @@ def tile_attend_gedgew_kernel(tc, W, hT, dyT, soffs, toffs, out):
         held = ctx.enter_context(tc.tile_pool(name="held", bufs=1))
         psum = ctx.enter_context(tc.psum_pool(name="psum", bufs=1))
 
+        def tile(shape, dtype, name, tag=None):
+            return held.tile(shape, dtype, name=name, tag=tag or name, align_bytes=64)
+
         toffs_t = held.tile([P, C // 16], U16, name="toffs_t")
         soffs_t = held.tile([P, C // 16], U16, name="soffs_t")
-        dy = [held.tile([P, WINDOW], F32, name="dy%d" % b) for b in range(BLOCKS)]
-        u = [held.tile([P, WINDOW], F32, name="u%d" % b) for b in range(BLOCKS)]
-        h_raw = [
-            held.tile([P, PACK, HALF], F32, name="h_raw%d" % i, tag="h_raw%d" % i, align_bytes=64) for i in range(2)
-        ]
-        w_cols = [slice(0, P), slice(P, HALF), slice(HALF, M)]
-        w_raw = [
-            held.tile([P, PACK, c.stop - c.start], F32, name="w_raw%d" % i, tag="w_raw%d" % i, align_bytes=64)
-            for i, c in enumerate(w_cols)
-        ]
+        dy = [tile([P, WINDOW if b else WIDE_WINDOW], F32, "dy%d" % b) for b in range(BLOCKS)]
+        u = [tile([P, WINDOW], F32, "u%d" % b) for b in range(BLOCKS)]
+        h_raw = tile([P, PACK, X], F32, "h_raw")
+        w_raw = [tile([P, PACK, HALF], F32, "w_raw%d" % i) for i in range(2)]
         w_rows = W.rearrange("(p j) m -> p j m", j=PACK)
-        h_rows = hT.rearrange("(p j) x -> p j x", j=PACK)
 
         def load_dy(b):
             nc.sync.dma_start(dy[b][:, 0:X], dyT[b * P : (b + 1) * P, :])
@@ -53,101 +53,119 @@ def tile_attend_gedgew_kernel(tc, W, hT, dyT, soffs, toffs, out):
         nc.sync.dma_start(toffs_t[:], toffs)
         load_dy(0)
         load_dy(1)
-        nc.sync.dma_start(h_raw[0][:], h_rows[:, :, 0:HALF])
-        nc.sync.dma_start(w_raw[0][:], w_rows[:, :, w_cols[0]])
-        nc.sync.dma_start(h_raw[1][:], h_rows[:, :, HALF:X])
-        nc.sync.dma_start(w_raw[1][:], w_rows[:, :, w_cols[1]])
-        nc.sync.dma_start(w_raw[2][:], w_rows[:, :, w_cols[2]])
+        nc.sync.dma_start(h_raw[:], hT.rearrange("(p j) x -> p j x", j=PACK))
+        nc.sync.dma_start(w_raw[0][:], w_rows[:, :, 0:HALF])
         nc.sync.dma_start(soffs_t[:], soffs)
+        nc.sync.dma_start(w_raw[1][:], w_rows[:, :, HALF:M])
         load_dy(2)
         load_dy(3)
 
-        ident = held.tile([P, P], F32, name="ident")
+        ident = tile([P, P], F32, "ident")
         make_identity(nc, ident[:])
-        sums = [held.tile([P, SQ], F32, name="sums%d" % i, align_bytes=64) for i in range(len(SETS))]
-        nc.vector.memset(sums[0][:], 0.0)
-        for later in sums[1:]:
-            nc.scalar.copy(later[:], sums[0][:])
+        sums = tile([P, 2 * SQ], F32, "sums")
+        nc.vector.memset(sums[:, 0:SQ], 0.0)
+        nc.scalar.copy(sums[:, SQ : 2 * SQ], sums[:, 0:SQ])
 
-        h_codes = held.tile([P, X], U32, name="h_codes", tag="h_codes", align_bytes=64)
-        h_scales = held.tile([P, X], U8, name="h_scales", align_bytes=64)
-        w_codes = held.tile([P, M], U32, name="w_codes", tag="w_codes", align_bytes=64)
-        w_scales = held.tile([P, M], U8, name="w_scales", align_bytes=64)
-
-        def interleave(move, raw, grouped):
+        def rounded(move, raw, name, tag=None):
+            grouped = tile([P, raw.shape[2], PACK], BF16, name, tag)
             move(
-                out=grouped.rearrange("p (c i) t -> p c t i", i=4),
+                out=grouped[:].rearrange("p (c i) t -> p c t i", i=4),
                 in_=raw.rearrange("p t (c i) -> p c t i", i=4),
             )
+            return grouped
 
-        def grouped_tile(width, name, tag=None):
-            return held.tile([P, width, PACK], BF16, name=name, tag=tag or name, align_bytes=64)
-
-        def quantise(grouped, codes, scales):
+        def quantised(grouped, name, tag=None):
+            width = grouped.shape[1]
+            codes = tile([P, width], U32, name + "_codes", tag)
+            scales = tile([P, width], U8, name + "_scales")
             nc.vector.quantize_mx(
-                out=codes.bitcast(FP8X4), scales=scales, in_=grouped[:].rearrange("p w j -> p (w j)")
+                out=codes[:].bitcast(FP8X4), scales=scales[:], in_=grouped[:].rearrange("p w j -> p (w j)")
             )
+            return codes, scales
 
-        def multiply(b, lo, hi, bank):
-            acc = psum.tile([P, hi - lo], F32, name="acc%d_%d" % (b, lo), tag=bank)
-            mc = slice(b * P, (b + 1) * P)
-            nc.tensor.matmul_mx(
-                out=acc[:],
-                lhsT=w_codes[:, mc].bitcast(FP8X4),
-                lhsT_scale=w_scales[:, mc],
-                rhs=h_codes[:, lo:hi].bitcast(FP8X4),
-                rhs_scale=h_scales[:, lo:hi],
-                start=True,
-                stop=True,
-            )
+        def multiply(w, first, h, bank):
+            acc = psum.tile([P, X], F32, name="acc_" + bank, tag=bank)
+            mc = slice(first, first + P)
+            for i, (codes, scales) in h:
+                nc.tensor.matmul_mx(
+                    out=acc[:, i * HALF : (i + 1) * HALF],
+                    lhsT=w[0][:, mc].bitcast(FP8X4),
+                    lhsT_scale=w[1][:, mc],
+                    rhs=codes[:].bitcast(FP8X4),
+                    rhs_scale=scales[:],
+                    start=True,
+                    stop=True,
+                )
             return acc
 
         def edges(offsets, lo, hi):
             return offsets[:, lo // 16 : hi // 16]
 
-        def scalar_gather(window, offsets, lo, hi, name, tag=None):
-            picked = held.tile([P, hi - lo], F32, name=name, tag=tag or name, align_bytes=64)
-            nc.scalar.activation(picked[:], window[:].indirect(edges(offsets, lo, hi)), copy)
+        def gathered(b, lo, hi, on_scalar, tag=None):
+            picked = tile([P, hi - lo], F32, "dg%d_%d" % (b, lo), tag)
+            looked_up = dy[b][:].indirect(edges(toffs_t, lo, hi))
+            if on_scalar:
+                nc.scalar.activation(picked[:], looked_up, copy)
+            else:
+                nc.vector.tensor_copy(picked[:], looked_up)
             return picked
 
-        dg0 = held.tile([P, C], F32, name="dg0")
-        nc.vector.tensor_copy(dg0[:, 0:SHARE], dy[0][:].indirect(edges(toffs_t, 0, SHARE)))
-        nc.scalar.activation(dg0[:, SHARE:C], dy[0][:].indirect(edges(toffs_t, SHARE, C)), copy)
-        dg1 = scalar_gather(dy[1], toffs_t, 0, C, "dg1")
+        dg0 = gathered(0, 0, C, False)
+        dg1 = gathered(1, 0, C, True)
 
-        h_grouped = [grouped_tile(HALF, "h_grouped%d" % i) for i in range(2)]
-        w_grouped = [grouped_tile(P, "w_grouped0")]
-        interleave(nc.vector.tensor_copy, h_raw[0][:], h_grouped[0][:])
-        interleave(nc.vector.tensor_copy, w_raw[0][:], w_grouped[0][:])
-        quantise(h_grouped[0], h_codes[:, 0:HALF], h_scales[:, 0:HALF])
-        quantise(w_grouped[0], w_codes[:, 0:P], w_scales[:, 0:P])
-        interleave(nc.vector.tensor_copy, h_raw[1][:, :, 0:P], h_grouped[1][:, 0:P, :])
-        interleave(nc.scalar.copy, h_raw[1][:, :, P:HALF], h_grouped[1][:, P:HALF, :])
-        quantise(h_grouped[1], h_codes[:, HALF:X], h_scales[:, HALF:X])
-        nc.scalar.copy(out=u[0][:, 0:HALF], in_=multiply(0, 0, HALF, "bank0")[:])
-        w_grouped.append(grouped_tile(P, "w_grouped1", "h_raw1"))
-        interleave(nc.scalar.copy, w_raw[1][:], w_grouped[1][:])
-        quantise(w_grouped[1], w_codes[:, P:HALF], w_scales[:, P:HALF])
-        nc.vector.tensor_copy(out=u[0][:, HALF:X], in_=multiply(0, HALF, X, "bank1")[:])
-        w_grouped.append(grouped_tile(HALF, "w_grouped2", "w_raw1"))
-        interleave(nc.scalar.copy, w_raw[2][:], w_grouped[2][:])
-        nc.scalar.copy(out=u[1][:, 0:X], in_=multiply(1, 0, X, "bank2")[:])
-        dg2 = scalar_gather(dy[2], toffs_t, 0, C, "dg2", tag="w_raw2")
-
-        turned = [
-            psum.tile([P, len(members), P], F32, name="turned%d" % i, tag="bank%d" % (5 + i))
-            for i, members in enumerate(SETS)
+        h_grouped = [
+            rounded(nc.vector.tensor_copy, h_raw[:, :, i * HALF : (i + 1) * HALF], "h_grouped%d" % i) for i in range(2)
         ]
+        w_grouped = [rounded(nc.scalar.copy, w_raw[0][:, :, i * P : (i + 1) * P], "w_grouped%d" % i) for i in range(2)]
+        h0 = quantised(h_grouped[0], "h0")
+        w0 = quantised(w_grouped[0], "w0", "h_raw")
+        h1 = quantised(h_grouped[1], "h1")
+        w_grouped.append(rounded(nc.vector.tensor_copy, w_raw[1][:], "w_grouped2", "w_grouped0"))
+        w1 = quantised(w_grouped[1], "w1", "h_grouped1")
+        w2 = quantised(w_grouped[2], "w2")
+        h = [(0, h0), (1, h1)]
+        for i in range(2):
+            acc = multiply(w0, 0, h[i : i + 1], "bank%d" % i)
+            nc.scalar.copy(out=u[0][:, i * HALF : (i + 1) * HALF], in_=acc[:, i * HALF : (i + 1) * HALF])
+        nc.scalar.copy(out=u[1][:, 0:X], in_=multiply(w1, 0, h, "bank2")[:])
+
+        turned = {}
+
+        def open_bank(members):
+            i = BANKS.index(members)
+            bank = psum.tile([P, len(members), P], F32, name="turned%d" % i, tag="bank%d" % ((5 + i) % 8))
+            for g in members:
+                turned[g] = bank[:, g - members[0], :]
+
         out_rows = out.rearrange("o (g q j) -> (o g) q j", q=4, j=SQ)
 
-        def add_up(q, b, lo, hi):
+        def close(members):
+            for g in members:
+                which = [g in chosen for chosen in SETS].index(True)
+                column = sums[:, SUM_AT[g] : SUM_AT[g] + 1]
+                if which > 0:
+                    nc.vector.tensor_reduce(column, turned[g], mybir.AxisListType.X, add)
+                else:
+                    junk = tile([P, P], F32, "junk%d" % g)
+                    nc.scalar.activation(junk[:], turned[g], copy, accum_out=column)
+                if g == SETS[which][-1]:
+                    res = tile([P, SQ], F32, "res%d" % g)
+                    nc.vector.transpose(res[:], sums[:, TURN_AT[which] : TURN_AT[which] + SQ])
+                    for r in SETS[which]:
+                        queue = nc.scalar if r in ON_SCALAR_QUEUE else nc.sync
+                        queue.dma_start(out_rows[r], res[SUM_AT[r] - TURN_AT[which] : P : SQ, :])
+
+        def product(b, lo, hi, picked, tag=None):
+            q = tile([P, hi - lo], F32, "q%d_%d" % (b, lo), tag)
+            nc.vector.tensor_tensor(q[:], u[b][:].indirect(edges(soffs_t, lo, hi)), picked, mult)
             for k in range((hi - lo) // P):
                 g = lo // P + k
-                which = [g in members for members in SETS].index(True)
-                members = SETS[which]
+                members = [chosen for chosen in BANKS if g in chosen][0]
                 closes = b == BLOCKS - 1 and g == members[-1]
+                if g not in turned:
+                    open_bank(members)
                 nc.tensor.matmul(
-                    turned[which][:, g - members[0], :],
+                    turned[g],
                     q[:, k * P : (k + 1) * P],
                     ident[:],
                     start=(b == 0 and g == members[0]),
@@ -155,42 +173,20 @@ def tile_attend_gedgew_kernel(tc, W, hT, dyT, soffs, toffs, out):
                     is_transpose=True,
                 )
                 if closes:
-                    close(which)
+                    close(members)
+            return q
 
-        def close(which):
-            members = SETS[which]
-            if which == len(SETS) - 1:
-                nc.vector.tensor_reduce(sums[which][:, 0 : len(members)], turned[which][:], mybir.AxisListType.X, add)
-            else:
-                for k, g in enumerate(members):
-                    junk = held.tile([P, P], F32, name="junk%d" % g)
-                    nc.scalar.activation(junk[:], turned[which][:, k, :], copy, accum_out=sums[which][:, k : k + 1])
-            res = held.tile([P, SQ], F32, name="res%d" % which, align_bytes=64)
-            nc.vector.transpose(res[:], sums[which][:])
-            for k, g in enumerate(members):
-                queue = nc.scalar if g == 6 else nc.sync
-                queue.dma_start(out_rows[g], res[k:P:SQ, :])
-
-        def fused(b, lo, hi, picked, tag=None):
-            name = "q%d_%d" % (b, lo)
-            q = held.tile([P, hi - lo], F32, name=name, tag=tag or name, align_bytes=64)
-            nc.vector.tensor_tensor(q[:], u[b][:].indirect(edges(soffs_t, lo, hi)), picked, mult)
-            add_up(q, b, lo, hi)
-
-        fused(0, 0, MID, dg0[:, 0:MID])
-        quantise(w_grouped[2], w_codes[:, HALF:M], w_scales[:, HALF:M])
-        fused(0, MID, C, dg0[:, MID:C], tag="w_raw1")
         for b in (2, 3):
-            nc.scalar.copy(out=u[b][:, 0:X], in_=multiply(b, 0, X, "bank%d" % (b + 1))[:])
-        dg3a = scalar_gather(dy[3], toffs_t, 0, MID, "dg3a", tag="w_codes")
-        dg3b = scalar_gather(dy[3], toffs_t, MID, C, "dg3b", tag="h_codes")
-        ug3b = scalar_gather(u[3], soffs_t, MID, C, "ug3b")
-        fused(1, 0, C, dg1[:])
-        fused(2, 0, MID, dg2[:, 0:MID])
-        fused(3, 0, MID, dg3a[:])
-        fused(2, MID, C, dg2[:, MID:C])
-        for lo in (MID, MID + HALF):
-            q = held.tile([P, HALF], F32, name="q3_%d" % lo)
-            part = slice(lo - MID, lo - MID + HALF)
-            nc.vector.tensor_tensor(q[:], ug3b[:, part], dg3b[:, part], mult)
-            add_up(q, 3, lo, lo + HALF)
+            nc.scalar.copy(out=u[b][:, 0:X], in_=multiply(w2, (b - 2) * P, h, "bank%d" % (b + 1))[:])
+        product(0, 0, C, dg0[:], "w_grouped0")
+        dg2 = gathered(2, 0, C, True, "w2_codes")
+        dg3a = gathered(3, 0, 512, True, "h0_codes")
+        dg3b = gathered(3, 512, 768, True, "h1_codes")
+        dg3c = gathered(3, 768, 1024, True, "h1_scales")
+        product(1, 0, C, dg1[:], "w2_scales")
+        product(2, 0, 768, dg2[:, 0:768])
+        product(3, 0, 512, dg3a[:])
+        product(3, 512, 768, dg3b[:])
+        product(2, 768, C, dg2[:, 768:C], "h0_codes")
+        product(3, 768, 896, dg3c[:, 0:P])
+        product(3, 896, C, dg3c[:, P : 2 * P])

@@ -44,8 +44,7 @@ def tile_attend_gedgew_kernel(tc, W, hT, dyT, soffs, toffs, out):
         dy = [tile([P, WINDOW if b else WIDE_WINDOW], F32, "dy%d" % b) for b in range(BLOCKS)]
         u = [tile([P, WINDOW], F32, "u%d" % b) for b in range(BLOCKS)]
         h_raw = tile([P, PACK, X], F32, "h_raw")
-        w_raw = [tile([P, PACK, HALF], F32, "w_raw%d" % i) for i in range(2)]
-        w_rows = W.rearrange("(p j) m -> p j m", j=PACK)
+        w_raw = tile([P, PACK, M], F32, "w_raw")
 
         def load_dy(b):
             nc.sync.dma_start(dy[b][:, 0:X], dyT[b * P : (b + 1) * P, :])
@@ -54,9 +53,8 @@ def tile_attend_gedgew_kernel(tc, W, hT, dyT, soffs, toffs, out):
         load_dy(0)
         load_dy(1)
         nc.sync.dma_start(h_raw[:], hT.rearrange("(p j) x -> p j x", j=PACK))
-        nc.sync.dma_start(w_raw[0][:], w_rows[:, :, 0:HALF])
+        nc.sync.dma_start(w_raw[:], W.rearrange("(p j) m -> p j m", j=PACK))
         nc.sync.dma_start(soffs_t[:], soffs)
-        nc.sync.dma_start(w_raw[1][:], w_rows[:, :, HALF:M])
         load_dy(2)
         load_dy(3)
 
@@ -116,18 +114,23 @@ def tile_attend_gedgew_kernel(tc, W, hT, dyT, soffs, toffs, out):
         h_grouped = [
             rounded(nc.vector.tensor_copy, h_raw[:, :, i * HALF : (i + 1) * HALF], "h_grouped%d" % i) for i in range(2)
         ]
-        w_grouped = [rounded(nc.scalar.copy, w_raw[0][:, :, i * P : (i + 1) * P], "w_grouped%d" % i) for i in range(2)]
+        w_upper = rounded(nc.scalar.copy, w_raw[:, :, HALF:M], "w_upper")
         h0 = quantised(h_grouped[0], "h0")
-        w0 = quantised(w_grouped[0], "w0", "h_raw")
         h1 = quantised(h_grouped[1], "h1")
-        w_grouped.append(rounded(nc.vector.tensor_copy, w_raw[1][:], "w_grouped2", "w_grouped0"))
-        w1 = quantised(w_grouped[1], "w1", "h_grouped1")
-        w2 = quantised(w_grouped[2], "w2")
+        w_lower = [
+            rounded(nc.vector.tensor_copy, w_raw[:, :, i * P : (i + 1) * P], "w_lower%d" % i, "h_grouped%d" % i)
+            for i in range(2)
+        ]
+        w0 = quantised(w_lower[0], "w0")
+        w1 = quantised(w_lower[1], "w1")
         h = [(0, h0), (1, h1)]
-        for i in range(2):
+        for i, move in enumerate((nc.vector.tensor_copy, nc.scalar.copy)):
             acc = multiply(w0, 0, h[i : i + 1], "bank%d" % i)
-            nc.scalar.copy(out=u[0][:, i * HALF : (i + 1) * HALF], in_=acc[:, i * HALF : (i + 1) * HALF])
+            move(out=u[0][:, i * HALF : (i + 1) * HALF], in_=acc[:, i * HALF : (i + 1) * HALF])
         nc.scalar.copy(out=u[1][:, 0:X], in_=multiply(w1, 0, h, "bank2")[:])
+        w23 = quantised(w_upper, "w23", "h_grouped1")
+        for b in (2, 3):
+            nc.scalar.copy(out=u[b][:, 0:X], in_=multiply(w23, (b - 2) * P, h, "bank%d" % (b + 1))[:])
 
         turned = {}
 
@@ -176,14 +179,12 @@ def tile_attend_gedgew_kernel(tc, W, hT, dyT, soffs, toffs, out):
                     close(members)
             return q
 
-        for b in (2, 3):
-            nc.scalar.copy(out=u[b][:, 0:X], in_=multiply(w2, (b - 2) * P, h, "bank%d" % (b + 1))[:])
-        product(0, 0, C, dg0[:], "w_grouped0")
-        dg2 = gathered(2, 0, C, True, "w2_codes")
+        product(0, 0, C, dg0[:], "w_upper")
+        dg2 = gathered(2, 0, C, True, "h_grouped1")
         dg3a = gathered(3, 0, 512, True, "h0_codes")
         dg3b = gathered(3, 512, 768, True, "h1_codes")
         dg3c = gathered(3, 768, 1024, True, "h1_scales")
-        product(1, 0, C, dg1[:], "w2_scales")
+        product(1, 0, C, dg1[:], "w23_scales")
         product(2, 0, 768, dg2[:, 0:768])
         product(3, 0, 512, dg3a[:])
         product(3, 512, 768, dg3b[:])

@@ -19,11 +19,26 @@ WINDOW = C + 8
 WIDE_WINDOW = 1376
 SQ = 32
 MID = C // 2
-BANKS = [range(g, g + 1) for g in range(8)]
-SETS = [range(0, 6), range(6, 7), range(7, 8)]
-TURN_AT = [16, 0, 32]
-SUM_AT = [16, 17, 18, 19, 20, 21, 24, 40]
-ON_SCALAR_QUEUE = (4, 5, 6)
+EARLY = 768
+PLACES = {
+    "u1": 0,
+    "w_raw2": 4096,
+    "q0_640": 6656,
+    "dg3_0": 4672,
+    "dg3_512": 6720,
+    "ug": 7744,
+    "q_last": 7744,
+    "u2": 12288,
+    "junk0": 12288,
+    "junk1": 12800,
+    "junk2": 13312,
+    "junk3": 13824,
+}
+
+BANKS = [range(0, 1), range(1, 2), range(2, 3), range(3, 4), range(4, 6), range(6, 7), range(7, 8)]
+BANK_AT = [5, 6, 7, 0, 1, 2, 3]
+SETS = [range(0, 4), range(4, 8)]
+SUM_STEP = 8
 FLOPS = 2 * D * M * X + 2 * M * C
 
 
@@ -34,17 +49,21 @@ def tile_attend_gedgew_kernel(tc, W, hT, dyT, soffs, toffs, out):
     copy = mybir.ActivationFunctionType.Copy
     with ExitStack() as ctx:
         held = ctx.enter_context(tc.tile_pool(name="held", bufs=1))
+        placed = ctx.enter_context(tc.tile_pool(name="placed", bufs=1))
         psum = ctx.enter_context(tc.psum_pool(name="psum", bufs=1))
 
         def tile(shape, dtype, name, tag=None):
+            if name in PLACES:
+                return placed.tile(shape, dtype, name=name, offset=PLACES[name], align_bytes=64)
             return held.tile(shape, dtype, name=name, tag=tag or name, align_bytes=64)
 
         toffs_t = held.tile([P, C // 16], U16, name="toffs_t")
         soffs_t = held.tile([P, C // 16], U16, name="soffs_t")
         dy = [tile([P, WINDOW if b else WIDE_WINDOW], F32, "dy%d" % b) for b in range(BLOCKS)]
-        u = [tile([P, WINDOW], F32, "u%d" % b) for b in range(BLOCKS)]
         h_raw = tile([P, PACK, X], F32, "h_raw")
-        w_raw = tile([P, PACK, M], F32, "w_raw")
+        w_cols = [slice(0, P), slice(P, HALF), slice(HALF, M)]
+        w_raw = [tile([P, PACK, c.stop - c.start], F32, "w_raw%d" % i) for i, c in enumerate(w_cols)]
+        w_rows = W.rearrange("(p j) m -> p j m", j=PACK)
 
         def load_dy(b):
             nc.sync.dma_start(dy[b][:, 0:X], dyT[b * P : (b + 1) * P, :])
@@ -52,10 +71,12 @@ def tile_attend_gedgew_kernel(tc, W, hT, dyT, soffs, toffs, out):
         nc.sync.dma_start(toffs_t[:], toffs)
         load_dy(0)
         load_dy(1)
-        nc.sync.dma_start(h_raw[:], hT.rearrange("(p j) x -> p j x", j=PACK))
-        nc.sync.dma_start(w_raw[:], W.rearrange("(p j) m -> p j m", j=PACK))
         nc.sync.dma_start(soffs_t[:], soffs)
+        nc.sync.dma_start(h_raw[:], hT.rearrange("(p j) x -> p j x", j=PACK))
+        nc.sync.dma_start(w_raw[0][:], w_rows[:, :, w_cols[0]])
         load_dy(2)
+        nc.sync.dma_start(w_raw[1][:], w_rows[:, :, w_cols[1]])
+        nc.sync.dma_start(w_raw[2][:], w_rows[:, :, w_cols[2]])
         load_dy(3)
 
         ident = tile([P, P], F32, "ident")
@@ -99,8 +120,8 @@ def tile_attend_gedgew_kernel(tc, W, hT, dyT, soffs, toffs, out):
         def edges(offsets, lo, hi):
             return offsets[:, lo // 16 : hi // 16]
 
-        def gathered(b, lo, hi, on_scalar, tag=None):
-            picked = tile([P, hi - lo], F32, "dg%d_%d" % (b, lo), tag)
+        def gathered(b, lo, hi, on_scalar, tag=None, into=None):
+            picked = tile([P, hi - lo], F32, "dg%d_%d" % (b, lo), tag) if into is None else into[:, lo:hi]
             looked_up = dy[b][:].indirect(edges(toffs_t, lo, hi))
             if on_scalar:
                 nc.scalar.activation(picked[:], looked_up, copy)
@@ -114,53 +135,43 @@ def tile_attend_gedgew_kernel(tc, W, hT, dyT, soffs, toffs, out):
         h_grouped = [
             rounded(nc.vector.tensor_copy, h_raw[:, :, i * HALF : (i + 1) * HALF], "h_grouped%d" % i) for i in range(2)
         ]
-        w_upper = rounded(nc.scalar.copy, w_raw[:, :, HALF:M], "w_upper")
+        w_grouped = [rounded(nc.scalar.copy, w_raw[0][:], "w_grouped0")]
+        dg2a = gathered(2, 0, EARLY, True)
         h0 = quantised(h_grouped[0], "h0")
+        w0 = quantised(w_grouped[0], "w0", "h_raw")
         h1 = quantised(h_grouped[1], "h1")
-        w_lower = [
-            rounded(nc.vector.tensor_copy, w_raw[:, :, i * P : (i + 1) * P], "w_lower%d" % i, "h_grouped%d" % i)
-            for i in range(2)
-        ]
-        w0 = quantised(w_lower[0], "w0")
-        w1 = quantised(w_lower[1], "w1")
+        dg2b = gathered(2, EARLY, C, False, "w_grouped0")
         h = [(0, h0), (1, h1)]
+        u = [tile([P, WINDOW], F32, "u0")]
         for i, move in enumerate((nc.vector.tensor_copy, nc.scalar.copy)):
             acc = multiply(w0, 0, h[i : i + 1], "bank%d" % i)
             move(out=u[0][:, i * HALF : (i + 1) * HALF], in_=acc[:, i * HALF : (i + 1) * HALF])
-        nc.scalar.copy(out=u[1][:, 0:X], in_=multiply(w1, 0, h, "bank2")[:])
-        w23 = quantised(w_upper, "w23", "h_grouped1")
-        for b in (2, 3):
-            nc.scalar.copy(out=u[b][:, 0:X], in_=multiply(w23, (b - 2) * P, h, "bank%d" % (b + 1))[:])
+        w_grouped.extend(rounded(nc.scalar.copy, w_raw[i][:], "w_grouped%d" % i) for i in (1, 2))
 
         turned = {}
+        banks = {}
 
         def open_bank(members):
             i = BANKS.index(members)
-            bank = psum.tile([P, len(members), P], F32, name="turned%d" % i, tag="bank%d" % ((5 + i) % 8))
+            bank = psum.tile([P, len(members), P], F32, name="turned%d" % i, tag="bank%d" % BANK_AT[i])
+            banks[members[0]] = bank
             for g in members:
                 turned[g] = bank[:, g - members[0], :]
 
-        out_rows = out.rearrange("o (g q j) -> (o g) q j", q=4, j=SQ)
+        out_rows = out.rearrange("o (g q j) -> q (o g) j", q=4, j=SQ)
 
         def close(members):
-            for g in members:
-                which = [g in chosen for chosen in SETS].index(True)
-                column = sums[:, SUM_AT[g] : SUM_AT[g] + 1]
-                if which > 0:
-                    nc.vector.tensor_reduce(column, turned[g], mybir.AxisListType.X, add)
-                else:
+            first, last = members[0], members[-1]
+            columns = sums[:, first * SUM_STEP : last * SUM_STEP + 1 : SUM_STEP]
+            if first < 6:
+                for g in members:
                     junk = tile([P, P], F32, "junk%d" % g)
+                    column = sums[:, g * SUM_STEP : g * SUM_STEP + 1]
                     nc.scalar.activation(junk[:], turned[g], copy, accum_out=column)
-                if g == SETS[which][-1]:
-                    res = tile([P, SQ], F32, "res%d" % g)
-                    nc.vector.transpose(res[:], sums[:, TURN_AT[which] : TURN_AT[which] + SQ])
-                    for r in SETS[which]:
-                        queue = nc.scalar if r in ON_SCALAR_QUEUE else nc.sync
-                        queue.dma_start(out_rows[r], res[SUM_AT[r] - TURN_AT[which] : P : SQ, :])
+            else:
+                nc.vector.tensor_reduce(columns, banks[first][:], mybir.AxisListType.X, add)
 
-        def product(b, lo, hi, picked, tag=None):
-            q = tile([P, hi - lo], F32, "q%d_%d" % (b, lo), tag)
-            nc.vector.tensor_tensor(q[:], u[b][:].indirect(edges(soffs_t, lo, hi)), picked, mult)
+        def add_up(b, lo, hi, q):
             for k in range((hi - lo) // P):
                 g = lo // P + k
                 members = [chosen for chosen in BANKS if g in chosen][0]
@@ -177,17 +188,52 @@ def tile_attend_gedgew_kernel(tc, W, hT, dyT, soffs, toffs, out):
                 )
                 if closes:
                     close(members)
+
+        def sources(b, lo, hi):
+            return u[b][:].indirect(edges(soffs_t, lo, hi))
+
+        def dense_sources(b, lo, hi, dense):
+            nc.scalar.activation(dense, sources(b, lo, hi), copy)
+            return dense
+
+        def product(b, lo, hi, picked, tag=None, upto=None, dense=None, into=None):
+            q = tile([P, hi - lo], F32, "q%d_%d" % (b, lo), tag) if into is None else into
+            nc.vector.tensor_tensor(q[:], sources(b, lo, hi) if dense is None else dense, picked, mult)
+            add_up(b, lo, upto or hi, q)
             return q
 
-        product(0, 0, C, dg0[:], "w_upper")
-        dg2 = gathered(2, 0, C, True, "h_grouped1")
-        dg3a = gathered(3, 0, 512, True, "h0_codes")
-        dg3b = gathered(3, 512, 768, True, "h1_codes")
-        dg3c = gathered(3, 768, 1024, True, "h1_scales")
-        product(1, 0, C, dg1[:], "w23_scales")
-        product(2, 0, 768, dg2[:, 0:768])
+        def copied_out(b, w, first, tag=None):
+            u.append(tile([P, WINDOW], F32, "u%d" % b, tag))
+            nc.scalar.copy(out=u[b][:, 0:X], in_=multiply(w, first, h, "bank%d" % (b + 1))[:])
+
+        product(0, 0, 256, dg0[:, 0:256])
+        w1 = quantised(w_grouped[1], "w1")
+        copied_out(1, w1, 0)
+        product(0, 256, 640, dg0[:, 256:640], "w_raw1")
+        w23 = quantised(w_grouped[2], "w23")
+        dg3c = gathered(3, 768, C, True, "w_grouped2")
+        copied_out(2, w23, 0)
+        copied_out(3, w23, P)
+        product(0, 640, C, dg0[:, 640:C])
+        product(1, 0, C, dg1[:])
+        dg3a = gathered(3, 0, 512, True)
+        dg3b = gathered(3, 512, 768, True)
+        ug = tile([P, 256], F32, "ug")
+        ug3b = dense_sources(3, 512, 768, ug[:])
+        ug2 = tile([P, 256], F32, "ug2", "dg1_0")
+        ug2b = dense_sources(2, 768, C, ug2[:])
+        product(2, 0, 768, dg2a[:])
         product(3, 0, 512, dg3a[:])
-        product(3, 512, 768, dg3b[:])
-        product(2, 768, C, dg2[:, 768:C], "h0_codes")
-        product(3, 768, 896, dg3c[:, 0:P])
-        product(3, 896, C, dg3c[:, P : 2 * P])
+        product(3, 512, 768, dg3b[:], dense=ug3b)
+        product(2, 768, C, dg2b[:], dense=ug2b)
+        last = tile([P, 256], F32, "q_last")
+        product(3, 768, 896, dg3c[:, 0:P], into=last[:, 0:P])
+        product(3, 896, C, dg3c[:, P : 2 * P], into=last[:, P : 2 * P])
+        early = tile([P, SQ], F32, "res_early", "w_grouped2")
+        nc.vector.transpose(early[:], sums[:, 0:SQ])
+        for g in SETS[0]:
+            queue = nc.scalar if g % 2 else nc.sync
+            queue.dma_start(out_rows[:, g : g + 1, :], early[g * SUM_STEP : P : SQ, :])
+        late = tile([P, SQ], F32, "res_late")
+        nc.vector.transpose(late[:], sums[:, SQ : 2 * SQ])
+        nc.sync.dma_start(out_rows[:, SETS[1][0] : SETS[1][-1] + 1, :], late[0:P:SUM_STEP, :])

@@ -19,16 +19,13 @@ WINDOW = C + 8
 WIDE_WINDOW = 1376
 SQ = 32
 MID = C // 2
-EARLY = 768
+EARLY = 384
 PLACES = {
     "u1": 0,
     "w_raw2": 4096,
     "q0_640": 6656,
-    "dg3_0": 4672,
-    "dg3_512": 6720,
-    "ug": 7744,
-    "q_last": 7744,
-    "u2": 12288,
+    "dg3_0": 6656,
+    "dy3": 12288,
     "junk0": 12288,
     "junk1": 12800,
     "junk2": 13312,
@@ -130,7 +127,9 @@ def tile_attend_gedgew_kernel(tc, W, hT, dyT, soffs, toffs, out):
             return picked
 
         dg0 = gathered(0, 0, C, False)
-        dg1 = gathered(1, 0, C, True)
+        dg1 = tile([P, C], F32, "dg1")
+        gathered(1, 0, 768, True, into=dg1)
+        gathered(1, 768, C, False, into=dg1)
 
         h_grouped = [
             rounded(nc.vector.tensor_copy, h_raw[:, :, i * HALF : (i + 1) * HALF], "h_grouped%d" % i) for i in range(2)
@@ -140,13 +139,14 @@ def tile_attend_gedgew_kernel(tc, W, hT, dyT, soffs, toffs, out):
         h0 = quantised(h_grouped[0], "h0")
         w0 = quantised(w_grouped[0], "w0", "h_raw")
         h1 = quantised(h_grouped[1], "h1")
-        dg2b = gathered(2, EARLY, C, False, "w_grouped0")
+        dg2c = gathered(2, 768, C, False, "w_grouped0")
         h = [(0, h0), (1, h1)]
         u = [tile([P, WINDOW], F32, "u0")]
         for i, move in enumerate((nc.vector.tensor_copy, nc.scalar.copy)):
             acc = multiply(w0, 0, h[i : i + 1], "bank%d" % i)
             move(out=u[0][:, i * HALF : (i + 1) * HALF], in_=acc[:, i * HALF : (i + 1) * HALF])
-        w_grouped.extend(rounded(nc.scalar.copy, w_raw[i][:], "w_grouped%d" % i) for i in (1, 2))
+        w_grouped.append(rounded(nc.vector.tensor_copy, w_raw[1][:], "w_grouped1", "w0_codes"))
+        w_grouped.append(rounded(nc.scalar.copy, w_raw[2][:], "w_grouped2"))
 
         turned = {}
         banks = {}
@@ -206,30 +206,28 @@ def tile_attend_gedgew_kernel(tc, W, hT, dyT, soffs, toffs, out):
             u.append(tile([P, WINDOW], F32, "u%d" % b, tag))
             nc.scalar.copy(out=u[b][:, 0:X], in_=multiply(w, first, h, "bank%d" % (b + 1))[:])
 
-        product(0, 0, 256, dg0[:, 0:256])
         w1 = quantised(w_grouped[1], "w1")
         copied_out(1, w1, 0)
-        product(0, 256, 640, dg0[:, 256:640], "w_raw1")
+        product(0, 0, 640, dg0[:, 0:640], "w_raw1")
         w23 = quantised(w_grouped[2], "w23")
-        dg3c = gathered(3, 768, C, True, "w_grouped2")
+        dg2b = gathered(2, EARLY, 768, True, "w_grouped2")
         copied_out(2, w23, 0)
         copied_out(3, w23, P)
         product(0, 640, C, dg0[:, 640:C])
         product(1, 0, C, dg1[:])
-        dg3a = gathered(3, 0, 512, True)
-        dg3b = gathered(3, 512, 768, True)
-        ug = tile([P, 256], F32, "ug")
-        ug3b = dense_sources(3, 512, 768, ug[:])
-        ug2 = tile([P, 256], F32, "ug2", "dg1_0")
-        ug2b = dense_sources(2, 768, C, ug2[:])
-        product(2, 0, 768, dg2a[:])
-        product(3, 0, 512, dg3a[:])
-        product(3, 512, 768, dg3b[:], dense=ug3b)
-        product(2, 768, C, dg2b[:], dense=ug2b)
-        last = tile([P, 256], F32, "q_last")
-        product(3, 768, 896, dg3c[:, 0:P], into=last[:, 0:P])
-        product(3, 896, C, dg3c[:, P : 2 * P], into=last[:, P : 2 * P])
-        early = tile([P, SQ], F32, "res_early", "w_grouped2")
+        dg3a = gathered(3, 0, MID, True)
+        dg3b = gathered(3, MID, 768, True, "q1_0")
+        product(2, 0, EARLY, dg2a[:])
+        ug2 = tile([P, 256], F32, "ug2", "dg2_0")
+        ug2c = dense_sources(2, 768, C, ug2[:])
+        product(2, EARLY, 768, dg2b[:])
+        dg3c = gathered(3, 768, C, True, "q2_384")
+        product(3, 0, MID, dg3a[:])
+        product(3, MID, 768, dg3b[:])
+        product(2, 768, C, dg2c[:], dense=ug2c)
+        product(3, 768, 896, dg3c[:, 0:P])
+        product(3, 896, C, dg3c[:, P : 2 * P])
+        early = tile([P, SQ], F32, "res_early", "q2_384")
         nc.vector.transpose(early[:], sums[:, 0:SQ])
         for g in SETS[0]:
             queue = nc.scalar if g % 2 else nc.sync

@@ -127,9 +127,7 @@ def tile_attend_gedgew_kernel(tc, W, hT, dyT, soffs, toffs, out):
             return picked
 
         dg0 = gathered(0, 0, C, False)
-        dg1 = tile([P, C], F32, "dg1")
-        gathered(1, 0, 768, True, into=dg1)
-        gathered(1, 768, C, False, into=dg1)
+        dg1 = gathered(1, 0, C, True)
 
         h_grouped = [
             rounded(nc.vector.tensor_copy, h_raw[:, :, i * HALF : (i + 1) * HALF], "h_grouped%d" % i) for i in range(2)
@@ -142,9 +140,9 @@ def tile_attend_gedgew_kernel(tc, W, hT, dyT, soffs, toffs, out):
         dg2c = gathered(2, 768, C, False, "w_grouped0")
         h = [(0, h0), (1, h1)]
         u = [tile([P, WINDOW], F32, "u0")]
-        for i, move in enumerate((nc.vector.tensor_copy, nc.scalar.copy)):
+        for i in range(2):
             acc = multiply(w0, 0, h[i : i + 1], "bank%d" % i)
-            move(out=u[0][:, i * HALF : (i + 1) * HALF], in_=acc[:, i * HALF : (i + 1) * HALF])
+            nc.scalar.copy(out=u[0][:, i * HALF : (i + 1) * HALF], in_=acc[:, i * HALF : (i + 1) * HALF])
         w_grouped.append(rounded(nc.vector.tensor_copy, w_raw[1][:], "w_grouped1", "w0_codes"))
         w_grouped.append(rounded(nc.scalar.copy, w_raw[2][:], "w_grouped2"))
 

@@ -23,13 +23,12 @@ EARLY = 384
 PLACES = {
     "u1": 0,
     "w_raw2": 4096,
-    "q0_640": 6656,
-    "dg3_0": 6656,
+    "q0_640": 8192,
+    "dg3_0": 8192,
+    "q_last": 8192,
     "dy3": 12288,
-    "junk0": 12288,
-    "junk1": 12800,
-    "junk2": 13312,
-    "junk3": 13824,
+    "u2": 16448,
+    "junk": 15360,
 }
 
 BANKS = [range(0, 1), range(1, 2), range(2, 3), range(3, 4), range(4, 6), range(6, 7), range(7, 8)]
@@ -68,11 +67,11 @@ def tile_attend_gedgew_kernel(tc, W, hT, dyT, soffs, toffs, out):
         nc.sync.dma_start(toffs_t[:], toffs)
         load_dy(0)
         load_dy(1)
-        nc.sync.dma_start(soffs_t[:], soffs)
         nc.sync.dma_start(h_raw[:], hT.rearrange("(p j) x -> p j x", j=PACK))
         nc.sync.dma_start(w_raw[0][:], w_rows[:, :, w_cols[0]])
         load_dy(2)
         nc.sync.dma_start(w_raw[1][:], w_rows[:, :, w_cols[1]])
+        nc.sync.dma_start(soffs_t[:], soffs)
         nc.sync.dma_start(w_raw[2][:], w_rows[:, :, w_cols[2]])
         load_dy(3)
 
@@ -158,14 +157,21 @@ def tile_attend_gedgew_kernel(tc, W, hT, dyT, soffs, toffs, out):
 
         out_rows = out.rearrange("o (g q j) -> q (o g) j", q=4, j=SQ)
 
+        scratches = {}
+
+        def scratch(g):
+            late = g not in SETS[0]
+            if late not in scratches:
+                scratches[late] = tile([P, 4, P], F32, "junk_late" if late else "junk")
+            return scratches[late][:, g % 4, :]
+
         def close(members):
             first, last = members[0], members[-1]
             columns = sums[:, first * SUM_STEP : last * SUM_STEP + 1 : SUM_STEP]
             if first < 6:
                 for g in members:
-                    junk = tile([P, P], F32, "junk%d" % g)
                     column = sums[:, g * SUM_STEP : g * SUM_STEP + 1]
-                    nc.scalar.activation(junk[:], turned[g], copy, accum_out=column)
+                    nc.scalar.activation(scratch(g), turned[g], copy, accum_out=column)
             else:
                 nc.vector.tensor_reduce(columns, banks[first][:], mybir.AxisListType.X, add)
 
@@ -207,25 +213,26 @@ def tile_attend_gedgew_kernel(tc, W, hT, dyT, soffs, toffs, out):
         w1 = quantised(w_grouped[1], "w1")
         copied_out(1, w1, 0)
         product(0, 0, 640, dg0[:, 0:640], "w_raw1")
+        q0 = product(0, 640, C, dg0[:, 640:C], upto=896)
         w23 = quantised(w_grouped[2], "w23")
         dg2b = gathered(2, EARLY, 768, True, "w_grouped2")
         copied_out(2, w23, 0)
         copied_out(3, w23, P)
-        product(0, 640, C, dg0[:, 640:C])
+        add_up(0, 896, C, q0[:, 2 * P : 3 * P])
         product(1, 0, C, dg1[:])
         dg3a = gathered(3, 0, MID, True)
-        dg3b = gathered(3, MID, 768, True, "q1_0")
-        product(2, 0, EARLY, dg2a[:])
-        ug2 = tile([P, 256], F32, "ug2", "dg2_0")
+        ug2 = tile([P, 256], F32, "ug2", "dg1_0")
         ug2c = dense_sources(2, 768, C, ug2[:])
+        product(2, 0, EARLY, dg2a[:])
+        dg3b = gathered(3, MID, C, True, "dg2_0")
         product(2, EARLY, 768, dg2b[:])
-        dg3c = gathered(3, 768, C, True, "q2_384")
         product(3, 0, MID, dg3a[:])
-        product(3, MID, 768, dg3b[:])
         product(2, 768, C, dg2c[:], dense=ug2c)
-        product(3, 768, 896, dg3c[:, 0:P])
-        product(3, 896, C, dg3c[:, P : 2 * P])
-        early = tile([P, SQ], F32, "res_early", "q2_384")
+        product(3, MID, 768, dg3b[:, 0 : 2 * P])
+        last = tile([P, 256], F32, "q_last")
+        product(3, 768, 896, dg3b[:, 2 * P : 3 * P], into=last[:, 0:P])
+        product(3, 896, C, dg3b[:, 3 * P : 4 * P], into=last[:, P : 2 * P])
+        early = tile([P, SQ], F32, "res_early", "dg2_0")
         nc.vector.transpose(early[:], sums[:, 0:SQ])
         for g in SETS[0]:
             queue = nc.scalar if g % 2 else nc.sync

@@ -19,7 +19,7 @@ WINDOW = C + 8
 WIDE_WINDOW = 1376
 SQ = 32
 MID = C // 2
-EARLY = 384
+EARLY = 512
 PLACES = {
     "u1": 0,
     "w_raw2": 4096,
@@ -136,7 +136,7 @@ def tile_attend_gedgew_kernel(tc, W, hT, dyT, soffs, toffs, out):
         h0 = quantised(h_grouped[0], "h0")
         w0 = quantised(w_grouped[0], "w0", "h_raw")
         h1 = quantised(h_grouped[1], "h1")
-        dg2c = gathered(2, 768, C, False, "w_grouped0")
+        dg2c = gathered(2, EARLY, C, False, "w_grouped0")
         h = [(0, h0), (1, h1)]
         u = [tile([P, WINDOW], F32, "u0")]
         for i in range(2):
@@ -215,7 +215,7 @@ def tile_attend_gedgew_kernel(tc, W, hT, dyT, soffs, toffs, out):
         product(0, 0, 640, dg0[:, 0:640], "w_raw1")
         q0 = product(0, 640, C, dg0[:, 640:C], upto=896)
         w23 = quantised(w_grouped[2], "w23")
-        dg2b = gathered(2, EARLY, 768, True, "w_grouped2")
+        dg3c = gathered(3, 768, C, True, "w_grouped2")
         copied_out(2, w23, 0)
         copied_out(3, w23, P)
         add_up(0, 896, C, q0[:, 2 * P : 3 * P])
@@ -224,15 +224,15 @@ def tile_attend_gedgew_kernel(tc, W, hT, dyT, soffs, toffs, out):
         ug2 = tile([P, 256], F32, "ug2", "dg1_0")
         ug2c = dense_sources(2, 768, C, ug2[:])
         product(2, 0, EARLY, dg2a[:])
-        dg3b = gathered(3, MID, C, True, "dg2_0")
-        product(2, EARLY, 768, dg2b[:])
+        dg3b = gathered(3, MID, 768, True, "dg2_0")
+        product(2, EARLY, 768, dg2c[:, 0 : 2 * P])
         product(3, 0, MID, dg3a[:])
-        product(2, 768, C, dg2c[:], dense=ug2c)
-        product(3, MID, 768, dg3b[:, 0 : 2 * P])
+        product(2, 768, C, dg2c[:, 2 * P : 4 * P], dense=ug2c)
+        product(3, MID, 768, dg3b[:])
         last = tile([P, 256], F32, "q_last")
-        product(3, 768, 896, dg3b[:, 2 * P : 3 * P], into=last[:, 0:P])
-        product(3, 896, C, dg3b[:, 3 * P : 4 * P], into=last[:, P : 2 * P])
-        early = tile([P, SQ], F32, "res_early", "dg2_0")
+        product(3, 768, 896, dg3c[:, 0:P], into=last[:, 0:P])
+        product(3, 896, C, dg3c[:, P : 2 * P], into=last[:, P : 2 * P])
+        early = tile([P, SQ], F32, "res_early", "w_grouped2")
         nc.vector.transpose(early[:], sums[:, 0:SQ])
         for g in SETS[0]:
             queue = nc.scalar if g % 2 else nc.sync

from contextlib import ExitStack

import concourse.mybir as mybir
from concourse.masks import make_identity

F32 = mybir.dt.float32
BF16 = mybir.dt.bfloat16
U32 = mybir.dt.uint32
U16 = mybir.dt.uint16
U8 = mybir.dt.uint8
FP8X4 = mybir.dt.float8_e4m3fn_x4

P = 128
PACK = 4
D, M, X, C = 512, 512, 512, 1024
HALF = 256
BLOCKS = M // P
WINDOW = C + 8
WIDE_WINDOW = 1376
SQ = 32
MID = C // 2
EARLY = 512
PLACES = {
    "u1": 0,
    "w_raw2": 4096,
    "q0_640": 8192,
    "dg3_0": 8192,
    "q_last": 8192,
    "dy3": 12288,
    "u2": 16448,
    "junk": 15360,
}

BANKS = [range(0, 1), range(1, 2), range(2, 3), range(3, 4), range(4, 6), range(6, 7), range(7, 8)]
BANK_AT = [5, 6, 7, 0, 1, 2, 3]
SETS = [range(0, 4), range(4, 8)]
SUM_STEP = 8
FLOPS = 2 * D * M * X + 2 * M * C


def tile_attend_gedgew_kernel(tc, W, hT, dyT, soffs, toffs, out):
    nc = tc.nc
    mult = mybir.AluOpType.mult
    add = mybir.AluOpType.add
    copy = mybir.ActivationFunctionType.Copy
    with ExitStack() as ctx:
        held = ctx.enter_context(tc.tile_pool(name="held", bufs=1))
        placed = ctx.enter_context(tc.tile_pool(name="placed", bufs=1))
        psum = ctx.enter_context(tc.psum_pool(name="psum", bufs=1))

        def tile(shape, dtype, name, tag=None):
            if name in PLACES:
                return placed.tile(shape, dtype, name=name, offset=PLACES[name], align_bytes=64)
            return held.tile(shape, dtype, name=name, tag=tag or name, align_bytes=64)

        toffs_t = held.tile([P, C // 16], U16, name="toffs_t")
        soffs_t = held.tile([P, C // 16], U16, name="soffs_t")
        dy = [tile([P, WINDOW if b else WIDE_WINDOW], F32, "dy%d" % b) for b in range(BLOCKS)]
        h_raw = tile([P, PACK, X], F32, "h_raw")
        w_cols = [slice(0, P), slice(P, HALF), slice(HALF, M)]
        w_raw = [tile([P, PACK, c.stop - c.start], F32, "w_raw%d" % i) for i, c in enumerate(w_cols)]
        w_rows = W.rearrange("(p j) m -> p j m", j=PACK)

        def load_dy(b):
            nc.sync.dma_start(dy[b][:, 0:X], dyT[b * P : (b + 1) * P, :])

        nc.sync.dma_start(toffs_t[:], toffs)
        load_dy(0)
        load_dy(1)
        nc.sync.dma_start(h_raw[:], hT.rearrange("(p j) x -> p j x", j=PACK))
        nc.sync.dma_start(w_raw[0][:], w_rows[:, :, w_cols[0]])
        load_dy(2)
        nc.sync.dma_start(w_raw[1][:], w_rows[:, :, w_cols[1]])
        nc.sync.dma_start(soffs_t[:], soffs)
        nc.sync.dma_start(w_raw[2][:], w_rows[:, :, w_cols[2]])
        load_dy(3)

        ident = tile([P, P], F32, "ident")
        make_identity(nc, ident[:])
        sums = tile([P, 2 * SQ], F32, "sums")
        nc.vector.memset(sums[:, 0:SQ], 0.0)
        nc.scalar.copy(sums[:, SQ : 2 * SQ], sums[:, 0:SQ])

        def rounded(move, raw, name, tag=None):
            grouped = tile([P, raw.shape[2], PACK], BF16, name, tag)
            move(
                out=grouped[:].rearrange("p (c i) t -> p c t i", i=4),
                in_=raw.rearrange("p t (c i) -> p c t i", i=4),
            )
            return grouped

        def quantised(grouped, name, tag=None):
            width = grouped.shape[1]
            codes = tile([P, width], U32, name + "_codes", tag)
            scales = tile([P, width], U8, name + "_scales")
            nc.vector.quantize_mx(
                out=codes[:].bitcast(FP8X4), scales=scales[:], in_=grouped[:].rearrange("p w j -> p (w j)")
            )
            return codes, scales

        def multiply(w, first, h, bank):
            acc = psum.tile([P, X], F32, name="acc_" + bank, tag=bank)
            mc = slice(first, first + P)
            for i, (codes, scales) in h:
                nc.tensor.matmul_mx(
                    out=acc[:, i * HALF : (i + 1) * HALF],
                    lhsT=w[0][:, mc].bitcast(FP8X4),
                    lhsT_scale=w[1][:, mc],
                    rhs=codes[:].bitcast(FP8X4),
                    rhs_scale=scales[:],
                    start=True,
                    stop=True,
                )
            return acc

        def edges(offsets, lo, hi):
            return offsets[:, lo // 16 : hi // 16]

        def gathered(b, lo, hi, on_scalar, tag=None, into=None):
            picked = tile([P, hi - lo], F32, "dg%d_%d" % (b, lo), tag) if into is None else into[:, lo:hi]
            looked_up = dy[b][:].indirect(edges(toffs_t, lo, hi))
            if on_scalar:
                nc.scalar.activation(picked[:], looked_up, copy)
            else:
                nc.vector.tensor_copy(picked[:], looked_up)
            return picked

        dg0 = gathered(0, 0, C, False)
        dg1 = gathered(1, 0, C, True)

        h_grouped = [
            rounded(nc.vector.tensor_copy, h_raw[:, :, i * HALF : (i + 1) * HALF], "h_grouped%d" % i) for i in range(2)
        ]
        w_grouped = [rounded(nc.scalar.copy, w_raw[0][:], "w_grouped0")]
        dg2a = gathered(2, 0, EARLY, True)
        h0 = quantised(h_grouped[0], "h0")
        w0 = quantised(w_grouped[0], "w0", "h_raw")
        h1 = quantised(h_grouped[1], "h1")
        dg2c = gathered(2, EARLY, C, False, "w_grouped0")
        h = [(0, h0), (1, h1)]
        u = [tile([P, WINDOW], F32, "u0")]
        for i in range(2):
            acc = multiply(w0, 0, h[i : i + 1], "bank%d" % i)
            nc.scalar.copy(out=u[0][:, i * HALF : (i + 1) * HALF], in_=acc[:, i * HALF : (i + 1) * HALF])
        w_grouped.append(rounded(nc.vector.tensor_copy, w_raw[1][:], "w_grouped1", "w0_codes"))
        w_grouped.append(rounded(nc.scalar.copy, w_raw[2][:], "w_grouped2"))

        turned = {}
        banks = {}

        def open_bank(members):
            i = BANKS.index(members)
            bank = psum.tile([P, len(members), P], F32, name="turned%d" % i, tag="bank%d" % BANK_AT[i])
            banks[members[0]] = bank
            for g in members:
                turned[g] = bank[:, g - members[0], :]

        out_rows = out.rearrange("o (g q j) -> q (o g) j", q=4, j=SQ)

        scratches = {}

        def scratch(g):
            late = g not in SETS[0]
            if late not in scratches:
                scratches[late] = tile([P, 4, P], F32, "junk_late" if late else "junk")
            return scratches[late][:, g % 4, :]

        def close(members):
            first, last = members[0], members[-1]
            columns = sums[:, first * SUM_STEP : last * SUM_STEP + 1 : SUM_STEP]
            if first < 6:
                for g in members:
                    column = sums[:, g * SUM_STEP : g * SUM_STEP + 1]
                    nc.scalar.activation(scratch(g), turned[g], copy, accum_out=column)
            else:
                nc.vector.tensor_reduce(columns, banks[first][:], mybir.AxisListType.X, add)

        def add_up(b, lo, hi, q):
            for k in range((hi - lo) // P):
                g = lo // P + k
                members = [chosen for chosen in BANKS if g in chosen][0]
                closes = b == BLOCKS - 1 and g == members[-1]
                if g not in turned:
                    open_bank(members)
                nc.tensor.matmul(
                    turned[g],
                    q[:, k * P : (k + 1) * P],
                    ident[:],
                    start=(b == 0 and g == members[0]),
                    stop=closes,
                    is_transpose=True,
                )
                if closes:
                    close(members)

        def sources(b, lo, hi):
            return u[b][:].indirect(edges(soffs_t, lo, hi))

        def dense_sources(b, lo, hi, dense):
            nc.scalar.activation(dense, sources(b, lo, hi), copy)
            return dense

        def product(b, lo, hi, picked, tag=None, upto=None, dense=None, into=None):
            q = tile([P, hi - lo], F32, "q%d_%d" % (b, lo), tag) if into is None else into
            nc.vector.tensor_tensor(q[:], sources(b, lo, hi) if dense is None else dense, picked, mult)
            add_up(b, lo, upto or hi, q)
            return q

        def copied_out(b, w, first, tag=None):
            u.append(tile([P, WINDOW], F32, "u%d" % b, tag))
            nc.scalar.copy(out=u[b][:, 0:X], in_=multiply(w, first, h, "bank%d" % (b + 1))[:])

        w1 = quantised(w_grouped[1], "w1")
        copied_out(1, w1, 0)
        product(0, 0, 640, dg0[:, 0:640], "w_raw1")
        q0 = product(0, 640, C, dg0[:, 640:C], upto=896)
        w23 = quantised(w_grouped[2], "w23")
        dg3c = gathered(3, 768, C, True, "w_grouped2")
        copied_out(2, w23, 0)
        copied_out(3, w23, P)
        add_up(0, 896, C, q0[:, 2 * P : 3 * P])
        product(1, 0, C, dg1[:])
        dg3a = gathered(3, 0, MID, True)
        ug2 = tile([P, 256], F32, "ug2", "dg1_0")
        ug2c = dense_sources(2, 768, C, ug2[:])
        product(2, 0, EARLY, dg2a[:])
        dg3b = gathered(3, MID, 768, True, "dg2_0")
        product(2, EARLY, 768, dg2c[:, 0 : 2 * P])
        product(3, 0, MID, dg3a[:])
        product(2, 768, C, dg2c[:, 2 * P : 4 * P], dense=ug2c)
        product(3, MID, 768, dg3b[:])
        last = tile([P, 256], F32, "q_last")
        product(3, 768, 896, dg3c[:, 0:P], into=last[:, 0:P])
        product(3, 896, C, dg3c[:, P : 2 * P], into=last[:, P : 2 * P])
        early = tile([P, SQ], F32, "res_early", "w_grouped2")
        nc.vector.transpose(early[:], sums[:, 0:SQ])
        for g in SETS[0]:
            queue = nc.scalar if g % 2 else nc.sync
            queue.dma_start(out_rows[:, g : g + 1, :], early[g * SUM_STEP : P : SQ, :])
        late = tile([P, SQ], F32, "res_late")
        nc.vector.transpose(late[:], sums[:, SQ : 2 * SQ])
        nc.sync.dma_start(out_rows[:, SETS[1][0] : SETS[1][-1] + 1, :], late[0:P:SUM_STEP, :])
